import numpy as np, ml_dtypes
CORES = [10,34,74,98]
N = 4
BF = ml_dtypes.bfloat16
def gentries(a):
    return np.ascontiguousarray(a.reshape(8, 16, -1).transpose(0, 2, 1)).reshape(8, -1)
def gtable(e):
    e = np.asarray(e); return np.ascontiguousarray(e.reshape(8, -1, 16).transpose(0, 2, 1)).reshape(128, -1).astype(np.int32)
W, LV, B, NB, Q, C = 64, 4, 64, 16, 4, 5440
K = NB * Q
SMIN, SMAX, DM, SH = 4, 56, 12, 9
CUTS = np.array([12, 24, 48]); BASE = np.array([0, 4096, 5120, 5376])
def tobf(v):
    return v.astype(np.float32).astype(BF)
def tolists(v):
    return np.stack([gtable(u) for u in v])
def tobox(x, y, s):
    return np.stack([x, y, s], axis=2).reshape(N, 8, 3 * B).astype(np.int32)
def setup_inputs(rng):
    v = rng.integers(0, 256, (N, 128, C), dtype=np.uint8) & rng.integers(0, 256, (N, 128, C), dtype=np.uint8)
    w = rng.integers(-8, 9, (N, 128, 3, NB // 2)); w = np.concatenate([w, -w], axis=3).reshape(N, 128, 3 * NB)
    n = np.arange(K) // Q; hb = 64 // NB
    sx = 4 * (n % 4) + rng.integers(0, 4, (N, 8, K)); sy = hb * (n // 4) + rng.integers(0, hb, (N, 8, K))
    lo = np.append(SMIN, CUTS); hi = np.append(CUTS - 1, SMAX); l = rng.integers(0, LV, (N, 8, B))
    s = rng.integers(lo[l], hi[l] + 1); x = rng.integers(0, W - s + 1); y = rng.integers(0, W - s + 1)
    return {"pyr": tobf(v), "head": tobf(w), "sx": tolists(sx), "sy": tolists(sy), "box": tobox(x, y, s)}
def setup_inputs_ends(rng):
    d = setup_inputs(rng); E = np.concatenate([[SMIN, SMAX], CUTS, CUTS - 1])
    s = E[(np.arange(B) + np.arange(8)[:, None] + np.arange(N)[:, None, None]) % len(E)]
    d["box"] = tobox((W - s) * rng.integers(0, 2, s.shape), (W - s) * rng.integers(0, 2, s.shape), s)
    d["sx"] = tolists(15 * rng.integers(0, 2, (N, 8, K))); d["sy"] = tolists(15 * rng.integers(0, 2, (N, 8, K))); return d
def setup_inputs_slow(rng):
    d = setup_inputs(rng); w = np.zeros((N, 8, 16, 3, NB)); i = np.arange(N)[:, None, None]; g = np.arange(8)[:, None]; c = np.arange(3)
    w[i, g, rng.integers(0, 16, (N, 8, 3)), c, rng.integers(0, NB, (N, 8, 3))] = np.array([-8, -1, 1, 8])[(i + g + c) % 4]
    d["head"] = tobf(w.reshape(N, 128, 3 * NB)); return d
def setup_inputs_twins(rng):
    d = setup_inputs(rng); b = d["box"].reshape(N, 8, 3, B)
    d["box"] = np.ascontiguousarray(np.broadcast_to(b[..., :1], b.shape)).reshape(N, 8, 3 * B); return d
def setup_inputs_push(rng):
    d = setup_inputs(rng); g = 8 * rng.choice(np.array([-1, 1]), (N, 8, 1, 3, 1)); g[:, 0] = 8; g[:, 1] = -8
    d["head"] = tobf(np.broadcast_to(g, (N, 8, 16, 3, NB)).reshape(N, 128, 3 * NB)); return d
def setup_inputs_spread(rng):
    d = setup_inputs(rng); v = np.minimum(rng.integers(0, 256, (N, 8, 16, C), dtype=np.uint8), rng.integers(0, 256, (N, 8, 1, C), dtype=np.uint8))
    d["pyr"] = tobf(v.reshape(N, 128, C)); w = rng.integers(-8, 9, (N, 128, 3 * NB)); d["head"] = tobf(w * (rng.random(w.shape) < 0.25))
    d["sx"] = tolists(rng.integers(0, 16, (N, 8, K))); d["sy"] = tolists(rng.integers(0, 16, (N, 8, K))); return d
def check_inputs(d):
    bad = []
    v = d["pyr"].astype(np.float32)
    if not np.all((v >= 0) & (v <= 255) & (v == np.floor(v))): bad.append("pyr")
    v = d["head"].astype(np.float32)
    if not np.all((v >= -8) & (v <= 8) & (v == np.floor(v))): bad.append("head")
    for a in ("sx", "sy"):
        if not np.all((d[a] >= 0) & (d[a] <= 15)): bad.append(a)
    b = d["box"].astype(np.int64).reshape(N, 8, 3, B); x, y, s = b[:, :, 0], b[:, :, 1], b[:, :, 2]
    if not np.all((s >= SMIN) & (s <= SMAX)): bad.append("size")
    if not np.all((x >= 0) & (y >= 0) & (x + s <= W) & (y + s <= W)): bad.append("box")
    return bad
def reference(pyr, head, sx, sy, box):
    P = [pyr[q].astype(np.float32).reshape(8, 16, C) for q in range(N)]
    H = [head[q].astype(np.float32).astype(np.int64).reshape(8, 16, 3, NB) for q in range(N)]
    ax = [gentries(sx[q]).astype(np.int64)[:, None, :] for q in range(N)]; ay = [gentries(sy[q]).astype(np.int64)[:, None, :] for q in range(N)]
    feat = np.zeros((N, 128, NB * B), BF); trail = np.zeros((N, 8, N, 3, B), np.float32)
    g = np.arange(8)[:, None, None]; ch = np.arange(16)[None, :, None]
    for r in range(N):
        b = box[r].astype(np.int64).reshape(8, 3, B); x, y, s = b[:, 0], b[:, 1], b[:, 2]
        for h in range(N):
            q = (r + h) % N
            l = np.zeros((8, B), np.int64)
            for t in CUTS: l = l + (s >= t)
            u = (16 * x[:, :, None] + ax[q] * s[:, :, None]) >> (4 + l[:, :, None])
            v = (16 * y[:, :, None] + ay[q] * s[:, :, None]) >> (4 + l[:, :, None])
            at = BASE[l][:, :, None] + v * (W >> l)[:, :, None] + u
            e = P[q][g, ch, at.reshape(8, 1, B * K)]
            m = np.max(e.reshape(8, 16, B, NB, Q), axis=4)
            d = np.einsum("gcbn,gcdn->gdb", m.astype(np.int64), H[q]) >> SH
            d = np.minimum(np.maximum(d, -DM), DM)
            s = np.minimum(np.maximum(s + d[:, 2], SMIN), SMAX)
            x = np.minimum(np.maximum(x + d[:, 0], 0), W - s)
            y = np.minimum(np.maximum(y + d[:, 1], 0), W - s)
            trail[r, :, h] = np.stack([x, y, s], axis=1)
        feat[r] = m.transpose(0, 1, 3, 2).reshape(128, NB * B).astype(BF)
    return {"feat": feat, "trail": trail.reshape(N, 8, 3 * N * B)}

@@ -1,0 +1,522 @@
+import math
+from concourse.bass import DstId, RemoteDMATransfer
+from concourse.mybir import AluOpType as A, ActivationFunctionType as AF
+
+N = 4
+SIM = 112
+BATCH = [22, 22, 20]
+ACT_SHARE = [0.72, 0.72, 0.72]
+GP = 12
+NCOPY = 1
+WAYS = 2
+NCH = 8
+PLANFOR = [(1800, 1.15, 50., 90.), (3000, 1.5, 60., 110.), (2500, 1.9, 60., 110.), (4200, 1.5, 80., 160.)]
+TRIES = 20000
+STEPS = [[("win", 1), ("win", 1), ("win", 1), ("win", 1)],
+         [("win", 1), ("win", 1), ("win", -2), ("win2", 0)],
+         [("win", 1), ("win", 0), ("win3", -1), ("win2", 0)]][NCOPY]
+COPIES = [[], [(1, "win2")], [(-1, "win3"), (1, "win2")]][NCOPY]
+NBT = len(BATCH)
+B0 = [sum(BATCH[:i]) for i in range(NBT)]
+MV = [8256, 7168, 2176, 1984]
+LV = [(0, 4096), (4096, 1024), (5120, 256), (5376, 64)]
+WIN = MV[0] - MV[3] + 4096
+BIG0 = MV[1] - MV[3]
+CW = (WIN - BIG0) // NCH
+SMALL = MV[2] - MV[3] + 256
+UM = 160
+NK = 10
+KF, KF2, KM, KU0, KU1, KV0, KV1, KCZ, KLO, KW = range(NK)
+KTAB = [(KF, 13, 14, 1, 0.5), (KF, 14, 15, 1, 0.25), (KF, 7, 16, 8, 0.125), (KF, 6, 7, 1, -38.0),
+        (KF2, 13, 14, 1, 0.75), (KF2, 14, 15, 1, 0.1875), (KF2, 15, 16, 1, 3 / 64), (KF2, 6, 7, 1, -47.25),
+        (KF2, 7, 8, 1, 1 / 64),
+        (KM, 13, 14, 1, 1088.0), (KM, 14, 15, 1, 4992.0), (KM, 15, 16, 1, 192.0), (KM, 6, 7, 1, -257024.0),
+        (KM, 7, 8, 1, -320.0),
+        (KU0, 0, 1, 1, 1.0), (KU0, 14, 15, 1, float(UM)), (KU0, 15, 16, 1, -127 / 256), (KU1, 2, 3, 1, 1 / 16),
+        (KV0, 4, 5, 1, 64.0), (KV0, 1, 2, 1, -31.75), (KV0, 5, 6, 1, 1.0), (KV1, 3, 4, 1, 4.0),
+        (KLO, 1, 10, 4, 1.0), (KLO, 6, 8, 1, 1.0), (KLO, 2, 4, 1, 4.0), (KLO, 8, 13, 4, 8.0), (KLO, 10, 12, 1, 56.0),
+        (KLO, 13, 14, 1, 52.0), (KLO, 14, 15, 1, 40.0), (KLO, 15, 16, 1, 16.0),
+        (KW, 0, 5, 1, 64.0), (KW, 8, 13, 4, 52.0), (KW, 13, 16, 1, 1.0),
+        (KCZ, 13, 14, 1, 12288.0), (KCZ, 14, 15, 1, -32.0), (KCZ, 15, 16, 1, 1 / 16)]
+
+BF = "bfloat16"
+SCRATCH = {"sxy": ("sbuf", [128, 16], "int32"), "bx": ("sbuf", [128, 64], "int32"), "pi": ("sbuf", [128, 4], "int32"),
+           "kc": ("sbuf", [128, 16], "float32"), "pf": ("sbuf", [128, 4], "float32"), "mg": ("sbuf", [128, 8], "float32"),
+           "tr": ("sbuf", [128, 64], "float32"), "ft": ("sbuf", [128, 16, 64], BF)}
+for _k, _n in dict(krow=16 * NK, zrow=256, icol=128, jrow=128, grow=128, g8=32, mkl=128, tmpl=256, l1=256, fm=64, cz=32, eg=128,
+                   pw=112, seg=16 * max(BATCH), i0=64, i1=64, ti=64).items():
+    SCRATCH[_k] = ("sbuf", [128, _n], BF)
+for _w in ["win"] + [_c[1] for _c in COPIES]:
+    for _k, _n in (("", WIN), ("wz", 384), ("ot", 1024), ("oh", 1024)):
+        SCRATCH[_k + _w] = ("sbuf", [128, _n], BF)
+for _i, _nb in enumerate(BATCH):
+    SCRATCH["pa%d" % _i] = ("psum", [128, 512], "float32")
+    SCRATCH["pb%d" % _i] = ("psum", [128, 512], "float32")
+    if not NCOPY:
+        SCRATCH["fc%d" % _i] = ("sbuf", [128, 16 * _nb], BF)
+        SCRATCH["fl%d" % _i] = ("sbuf", [128, 16 * _nb], BF)
+    for _h in range(N + 1):
+        SCRATCH["mb%d_%d" % (_h, _i)] = ("sbuf", [128, N * (-(-_nb // 8) * 8)], BF)
+    for _h in range(N):
+        SCRATCH["off%d_%d" % (_h, _i)] = ("sbuf", [128, 4 * _nb], "uint16")
+        for _k, _n in (("uv", 2), ("gt", 64), ("sc", 64), ("tt", 1)):
+            SCRATCH["%s%d_%d" % (_k, _h, _i)] = ("sbuf", [128, _n * _nb], BF)
+SEMAPHORES = (["cP", "cV", "cA", "cG", "dpyr", "dhd", "dsxy", "dbx", "dft", "dtr", "sent"]
+              + [x + c[1] for c in COPIES for x in ("small", "big")] + ["ch%d" % k for k in range(NCH)]
+              + ["ar%d_%d" % (h, i) for h in range(1, N + 1) for i in range(NBT)] + ["af%d" % i for i in range(NBT)])
+CY = 1.04
+
+
+def plan(ops):
+    n = len(ops)
+    q = ["VAPGYX".index(o["q"]) for o in ops]
+    pre = [set(o["deps"]) | set(o["after"]) for o in ops]
+    cases = [([[(d, l1 if q[d] == q[k] else l2) for d in o["deps"]] + [(d, 0.) for d in o["after"]] for k, o in enumerate(ops)],
+              [o["cost"] + o["ge"] * gc * CY + o["hp"] * hop for o in ops]) for hop, gc, l1, l2 in PLANFOR]
+    tail = [o["tail"] for o in ops]
+
+    def replay(order, case):
+        dep, cost = case
+        end, why, res, free, last = [0.] * n, [-1] * n, [False] * n, [0.] * 6, [-1] * 6
+        for k in order:
+            e = q[k]
+            t, w, r = free[e], last[e], True
+            for d, l in dep[k]:
+                if end[d] + l > t:
+                    t, w, r = end[d] + l, d, False
+            end[k], why[k], res[k] = t + cost[k], w, r
+            if e != 5:
+                free[e], last[e] = end[k] - tail[k], k
+        return end, why, res
+
+    dep, cost = cases[1]
+    end, free, order, todo = {}, [0.] * 6, [], list(range(n))
+    while todo:
+        best = None
+        for k in todo:
+            if all(d in end for d in pre[k]):
+                t = max([free[q[k]]] + [end[d] + l for d, l in dep[k]])
+                key = (t + ops[k]["late"], k)
+                if best is None or key < best[0]:
+                    best = (key, k, t)
+        _, k, t = best
+        end[k] = t + cost[k]
+        if q[k] != 5:
+            free[q[k]] = end[k] - tail[k]
+        order.append(k)
+        todo.remove(k)
+
+    seed = [12345]
+
+    def rnd():
+        seed[0] = (seed[0] * 1103515245 + 12345) % 2147483648
+        return (seed[0] >> 8) / 8388608.0
+
+    def value(o):
+        r = [replay(o, c) for c in cases]
+        return sum(max(x[0]) for x in r) / len(r), r
+
+    cur, runs = value(order)
+    low, kept = cur, order
+    for it in range(TRIES):
+        end, why, res = runs[int(rnd() * len(runs))]
+        k, crit = max(range(n), key=end.index if False else (lambda x: end[x])), []
+        while k >= 0:
+            if res[k] and why[k] >= 0 and why[k] not in pre[k]:
+                crit.append(k)
+            k = why[k]
+        b = crit[int(rnd() * len(crit))] if crit and rnd() > 0.25 else order[int(rnd() * n)]
+        pb = order.index(b)
+        same = [x for x in order[max(0, pb - 40):pb] if q[x] == q[b]]
+        if q[b] >= 4 or not same:
+            continue
+        a = same[-min(len(same), (1, 1, 1, 2, 3, 5)[int(rnd() * 6)])]
+        if ops[a]["tail"] > 1000:
+            continue
+        pa = order.index(a)
+        seg = order[pa:pb + 1]
+        if rnd() < 0.5:
+            grp = {b}
+            for x in reversed(seg[:-1]):
+                if any(x in pre[y] for y in grp):
+                    grp.add(x)
+            new = [x for x in seg if x in grp] + [x for x in seg if x not in grp]
+        else:
+            grp = {a}
+            for x in seg[1:]:
+                if pre[x] & grp:
+                    grp.add(x)
+            new = [x for x in seg if x not in grp] + [x for x in seg if x in grp]
+        if a in grp and b in grp:
+            continue
+        o2 = order[:pa] + new + order[pb + 1:]
+        val, r2 = value(o2)
+        if val < cur or rnd() < math.exp((cur - val) / (150.0 * (1 - it / TRIES) + 5)):
+            order, cur, runs = o2, val, r2
+            if cur < low:
+                low, kept = cur, order
+    return kept, [max(replay(kept, c)[0]) for c in cases], replay(kept, cases[1])[0]
+
+
+def routes(src, dst, c, topo):
+    own = topo.cores_of(src)
+    far = [x for x in own if topo.die(x) != topo.die(src)]
+    first = [[x for x in far if topo.may_write(x, dst)][0],
+             [x for x in own if topo.die(x) == topo.die(src) and x != src][0],
+             [x for x in far if not topo.may_write(x, dst)][0]]
+    ways = [[first[0]]]
+    for b in first[1:WAYS]:
+        ways.append([b, [x for x in range(SIM) if topo.mates(topo.chip(x), topo.chip(dst)) and topo.die(x) == topo.die(b)
+                         and topo.may_write(b, x) and topo.may_write(x, dst)][c]])
+    return ways
+
+
+def chunk(t, k):
+    return t[:, BIG0 + k * CW:BIG0 + (k + 1) * CW]
+
+
+def first_masks(src, dst, topo, j):
+    off = topo.engines(src, dst)
+    rest = [e for e in topo.engines(src, routes(src, dst, 0, topo)[0][0]) if e not in off]
+    sets = [rest, off] if j == 0 else [rest[:len(rest) // 2], rest[len(rest) // 2:]]
+    return [(sum(1 << e for e in s), len(s)) for s in sets]
+
+
+def helper(g, core, T, topo):
+    n = 0
+    for r in range(N):
+        src = T.cores[r]
+        for c, (d, wn) in enumerate(COPIES):
+            dst = T.cores[(r + d) % N]
+            for w, way in enumerate(routes(src, dst, c, topo)):
+                if core not in way:
+                    continue
+                p = way.index(core)
+                to = way[p + 1] if p + 1 < len(way) else dst
+                rid, pid, _ = topo.addr(to)
+                for k in range(w, NCH, WAYS):
+                    if p or c == 0:
+                        g.wait_ge(T.sem["ch%d" % k], len(topo.engines(way[0], core)) if p else first_masks(src, dst, topo, k // 2)[k % 2][1])
+                    g.remote_dma(chunk(T[wn] if to == dst else T.win, k), chunk(T.win, k),
+                                 T.sem["big" + wn] if to == dst else T.sem["ch%d" % k], T.sem.sent, pid, rid, topo.mask(core, to))
+                    n += len(topo.engines(core, to))
+    if n:
+        g.wait_ge(T.sem.sent, n)
+
+
+def build(g, T, topo, core):
+    V, S, P, Y = g.vector, g.scalar, g.tensor, g.sync
+    ops = []
+    rank = T.rank_of(core)
+
+    def peer(d):
+        return T.cores[(rank + d) % N]
+
+    def op(q, cost, deps, fn, late=0.0, sem=None, after=(), tail=0.0, ge=0, hp=0, drain=False):
+        ops.append(dict(q=q, cost=float(cost), deps=list(deps), fn=fn, late=late, sem=sem, after=list(after), tail=tail,
+                        ge=ge, hp=hp, drain=drain))
+        return len(ops) - 1
+
+    def v(n, deps, fn, late=0.0):
+        return op("V", max(64, n) * CY, deps, fn, late)
+
+    def act(n, deps, out, in_, scale=1.0, late=0.0):
+        return op("A", max(64, n) * CY, deps, lambda: S.activation(out, in_, AF.Copy, scale=scale), late)
+
+    def ts(n, deps, *a, late=0.0):
+        return v(n, deps, lambda: V.tensor_scalar(*a), late)
+
+    def fill(n, ap, val, deps=(), late=0.0):
+        return v(n, deps, lambda: V.memset(ap, val), late)
+
+    def mm(n, deps, calls, after=()):
+        def fn():
+            r = None
+            for c in calls:
+                r = P.matmul(*c)
+            return r
+        return op("P", n * CY, deps, fn, after=after)
+
+    def load(q, out, in_, sem, cost):
+        return op(q, cost, [], lambda: (S if q == "A" else Y).dma_start(out, in_), -1e4, sem=sem, tail=cost - 100)
+
+    kc = T.kc
+
+    def col(k):
+        return kc[:, k:k + 1]
+
+    load("A", T.sxy[:, 0:4], T.sx[:], ("dsxy", 16), 2000)
+    dsy = load("A", T.sxy[:, 4:8], T.sy[:], ("dsxy", 32), 2000)
+    dbx = load("A", T.bx[0:24, :], T.box[:], ("dbx", 16), 2000)
+    dhd = load("A", T.win[:, 64:112], T.head[:], ("dhd", 16), 2000)
+    for l, (a, n) in enumerate(LV):
+        dp = load("Y", T.win[:, MV[l] - MV[3]:MV[l] - MV[3] + n], T.pyr[:, a:a + n], ("dpyr", 16 * (l + 1)), 6500)
+
+    zk = fill(80, T.krow[0:1, :], 0.0)
+    zo = fill(64, T.zrow[0:1, 120:128], 1.0)
+    ze = fill(64, T.eg[:], 0.0)
+    ks = [zo, fill(64, T.zrow[0:1, 0:120], 0.0), fill(64, T.zrow[0:1, 128:256], 0.0)]
+    for j, (k, a, b, st, val) in enumerate(KTAB):
+        ap = T.krow[0:1, a * NK + k:(b - 1) * NK + k + 1:st * NK]
+        if j % 5 in (1, 3):
+            ks.append(act(1, [zk, zo], ap, T.zrow[0:1, 120:120 + len(range(a, b, st))], val))
+        else:
+            ks.append(fill(1, ap, val, [zk]))
+    mk = mm(1024, ks, [(T.pa0[:, 0:NK], T.zrow[0:1, 120 - 8 * t:248 - 8 * t], T.krow[0:1, t * NK:(t + 1) * NK], t == 0, t == 15)
+                       for t in range(16)])
+
+    lastg = []
+
+    def gi(ap, pat, base, cm, val=None, deps=()):
+        n = math.prod(c for _, c in pat)
+        if val is None:
+            def fn():
+                return g.iota(ap, pat, base, cm, allow_small_or_imprecise_dtypes=True)
+        else:
+            def fn():
+                return g.affine_select(ap, ap, pat, A.not_equal, val, base, cm)
+        lastg[:] = [op("G", 150 + 2 * n * CY, list(deps) + lastg, fn)]
+        return lastg[0]
+
+    eg = T.eg
+    ipi = gi(T.pi[:, 0:1], [[0, 1]], 0, 1)
+    iic = gi(T.icol[:], [[1, 128]], 0, 0)
+    ig8 = gi(T.g8[:], [[0, 4], [1, 8]], 0, 0)
+    ijr = gi(T.jrow[:], [[0, 8], [1, 16]], 0, 0)
+    igr = gi(T.grow[:], [[1, 8], [0, 16]], 0, 0)
+    gi(eg[64:128, 0:40], [[-1, 40]], 0, 1, 1.0, [ze])
+    gi(eg[64:128, 64:128], [[0, 8], [-1, 8]], -16, 1, -1.0)
+    gi(eg[0:32, 0:24], [[-1, 3], [-3, 8]], 0, 1, 1 / 512)
+    gi(eg[0:32, 24:40], [[1, 2], [-3, 8]], -2, 1, 1 / 512)
+    gi(eg[0:32, 64:128], [[0, 8], [-3, 8]], -2, 1, -1 / 512)
+    gi(eg[64:128, 0:40], [[0, 40]], -48, 1, -192.0)
+    EG = gi(eg[64:128, 64:128], [[0, 64]], -48, 1, 256.0)
+    iseg = gi(T.seg[:], [[0, 4 * max(BATCH)], [256, 4]], 0, 0)
+    zp = fill(64, T.pw[:], 0.0, late=2000)
+    for e, o in ((0, 0), (1, 32), (2, 16)):
+        PW = gi(T.pw[64:128, 9 + e:105:12], [[-1, 8]], -o, 1, 1.0, [zp])
+
+    p1 = ts(1, [ipi], T.pi[:, 1:2], T.pi[:, 0:1], 7, None, A.bitwise_and)
+    p2 = ts(1, [ipi], T.pi[:, 2:3], T.pi[:, 0:1], 112, None, A.bitwise_and)
+    p3 = v(1, [p1, p2], lambda: V.tensor_copy(T.pf[:, 1:3], T.pi[:, 1:3]))
+    pm8, p16 = T.pf[:, 1:2], T.pf[:, 2:3]
+    oi = fill(64, T.i0[:], 1.0)
+    kcp = v(64, [mk], lambda: V.tensor_copy(kc[:, 0:NK], T.pa0[:, 0:NK]), -500)
+    khi = ts(1, [kcp], col(NK), col(KLO), col(KW), None, A.add, late=-500)
+    d0 = ts(64, [dbx, oi], T.i0[0:24, :], T.bx[0:24, :], 191.0, 512.0, A.add, A.mult, late=-500)
+    FM = [ts(1, [kcp, p3, ig8], T.fm[:, a:b], T.g8[:, 0:b - a], pm8, col(k), A.is_equal, A.mult)
+          for a, b, k in ((0, 24, KF), (24, 40, KF2), (40, 48, KM))]
+    FM.append(fill(1, T.fm[:, 48:64], 0.0))
+    ml = ts(64, [p3, igr], T.mkl[:], T.grow[:], pm8, None, A.is_equal)
+    L1 = []
+    for j, (k0, k1) in enumerate(((KU0, KU1), (KV0, KV1))):
+        tm = T.tmpl[:, 128 * j:128 * j + 128]
+        t1 = ts(64, [kcp, ijr], tm, T.jrow[:], col(k1), col(k0), A.mult, A.add)
+        L1.append(v(256, [t1, ml], lambda j=j, tm=tm: V.tensor_tensor(T.l1[:, 128 * j:128 * j + 128], tm, T.mkl[:], A.mult)))
+    sco = ts(8, [dsy, p3], T.win[:, 112:120], T.sxy[:, 0:8], p16, None, A.add)
+    CZ = ts(24, [kcp, iic], T.cz[:, 0:24], T.icol[:, 0:24], 0.0, col(KCZ), A.mult, A.add)
+    mgk = ts(8, [p3, iic], T.mg[:], T.icol[:, 0:128:16], p16, None, A.is_equal)
+
+    def frame(wn, d1, d2, pyr, late):
+        win, ot, oh, wz = T[wn], T["ot" + wn], T["oh" + wn], T["wz" + wn]
+        ots = [ts(64, [d1, iic], ot[:, 128 * j:128 * j + 128], T.icol[:], win[:, 112 + j:113 + j], None, A.is_equal, late=late)
+               for j in range(8)]
+        o = [v(128, ots[2 * j:2 * j + 2], lambda j=j: V.transpose(oh[:, 256 * j:256 * j + 256], ot[:, 256 * j:256 * j + 256]), late)
+             for j in range(4)]
+        w = [act(48, [mgk, d2], wz[:, 48 * j:48 * j + 48], win[:, 64:112], T.mg[:, j:j + 1], late) for j in range(8)]
+        return win, oh, wz, o, w, pyr
+
+    pyr0 = [dp, dhd, sco, fill(1, T.win[:, 120:192], 0.0), fill(1, T.win[:, 6208:6272], 0.0)]
+    frames = {"win": frame("win", sco, dhd, pyr0, 0.0)}
+    nsent = [0]
+
+    def send(src, dst, to, sem, deps, cost, after=()):
+        rid, pid, _ = topo.addr(to)
+        nsent[0] += len(topo.engines(core, to))
+        s = op("G", 600, deps, lambda: g.remote_dma(dst, src, T.sem[sem], T.sem.sent, pid, rid, topo.mask(core, to)), sem=(), after=after)
+        return op("X", cost, [], None, sem=(sem, len(topo.engines(core, to))), after=[s], hp=1)
+
+    if COPIES:
+        ways = routes(core, peer(1), 0, topo)
+        last = []
+        small = {}
+        for j in range(NCH // 2):
+            ms = first_masks(core, peer(1), topo, j)
+
+            def fused(j=j, ms=ms):
+                trs = []
+                for w in range(2):
+                    k = 2 * j + w
+                    rid, pid, _ = topo.addr(ways[k % WAYS][0])
+                    trs.append(RemoteDMATransfer(dst_ids=[DstId(rid=rid, pnc=pid)], dma_engine_mask=ms[w][0],
+                                                 remote_sem=T.sem["ch%d" % k], src=chunk(T.win, k), dst=chunk(T.win, k)))
+                return g.remote_dma_fused(trs, local_sem=T.sem.sent)
+            nsent[0] += ms[0][1] + ms[1][1]
+            last = [op("G", 600, pyr0, fused, sem=(), after=last)]
+            if j < len(COPIES):
+                d, wn = COPIES[j]
+                small[wn] = send(T.win[:, 0:SMALL], T[wn][:, 0:SMALL], peer(d), "small" + wn, pyr0, 2500, last)
+                last = [small[wn] - 1]
+        for c, (d, wn) in enumerate(COPIES):
+            back = routes(peer(-d), core, c, topo)
+            nbig = sum(len(topo.engines(back[k % WAYS][-1], core)) for k in range(NCH))
+            big = op("X", 9000 + 6000 * c, [], None, sem=("big" + wn, nbig), after=last)
+            frames[wn] = frame(wn, small[wn], small[wn], [small[wn], big], 400.0)
+
+    def update(src, tt, pb, nb, deps):
+        mt = mm(64, deps + [EG], [(pb[:, 0:nb], eg[:], src, True, True)])
+        return ts(nb, [mt, khi], tt, pb[:, 0:nb], col(KLO), col(NK), A.max, A.min, late=-400)
+
+    def finish(dst_lo, dst_hi, tt, pa, nb, deps, last):
+        n4 = op("V", 60 + max(64, 2 * nb) * CY, deps, lambda: V.tensor_tensor(dst_hi, tt[0:64, :], tt[64:128, :], A.min), -400, drain=True)
+        if last:
+            return n4
+        mf = mm(64, deps + FM, [(pa[0:64, 0:nb], T.fm[:], tt[:], True, True)])
+        return v(nb, [n4, mf], lambda: V.tensor_tensor(dst_lo, dst_hi, pa[0:64, 0:nb], A.mult), -400)
+
+    init = finish(T.i1[0:64, :], T.i1[64:128, :], T.ti, T.pa0, 64, [update(T.i0[:], T.ti[:], T.pb0, 64, [d0])], False)
+
+    prev = [init] * NBT
+    bank = [init] * NBT
+    mbs = [T["mb0_%d" % i] for i in range(NBT)]
+    farr = [None] * NBT
+    hist = [None] * NBT
+    fo, to = [], []
+
+    def feat(i, src, step, deps):
+        nb = BATCH[i]
+        for n4 in range(4):
+            o, s = T.ft[:, n4:16:4, B0[i]:B0[i] + nb], src[:, (n4 + 1) * step - 1:16 * nb * step:4 * step]
+            fo.append(act(4 * nb, deps, o, s) if n4 % 2 else v(2 * nb, deps, lambda o=o, s=s: V.tensor_copy(o, s)))
+
+    def trail(i, hs, deps, after):
+        nb, w = BATCH[i], -(-BATCH[i] // 8) * 8
+        return mm(64 * len(hs), deps + [PW], [(T["pa%d" % i][0:96, 0:nb], T.pw[:, 9 - 3 * h:105 - 3 * h], mbs[i][:, h * w:h * w + nb],
+                                               h == 0, h == N - 1) for h in hs], after)
+
+    for h in range(N):
+        win, oh, wz, OH, WZ, pyr = frames[STEPS[h][0]]
+        for i, nb in enumerate(BATCH):
+            w = -(-nb // 8) * 8
+            pa, pb, mb = T["pa%d" % i], T["pb%d" % i], mbs[i]
+            uv, off, gt, sc, tt = (T["%s%d_%d" % (x, h, i)] for x in ("uv", "off", "gt", "sc", "tt"))
+            sb, sa = (T.i1, B0[i]) if h == 0 else (mb, (h - 1) * w)
+            src = sb[:, sa:sa + nb]
+            oa = h * w
+            clr = [fill(1, mb[:, oa:oa + w], 0.0, late=1000)] if h == N - 1 or w != nb else []
+            m1 = mm(128, [prev[i], bank[i]] + L1, [(pb[:, 0:nb], T.l1[:, 0:128], src, True, True),
+                                                   (pb[:, nb:2 * nb], T.l1[:, 128:256], src, True, True)])
+            rd = v(2 * nb, [m1], lambda uv=uv, pb=pb, nb=nb: V.tensor_copy(uv[:], pb[:, 0:2 * nb]), -300)
+            cv = []
+            for hf, ps in enumerate((pa, pb)):
+                calls = []
+                for k in range(2):
+                    nh = 2 * hf + k
+                    o = ps[:, k * nb:(k + 1) * nb]
+                    calls.append((o, oh[:, 128 * nh:128 * nh + 128], uv[:, 0:nb], True, False))
+                    calls.append((o, oh[:, 512 + 128 * nh:640 + 128 * nh], uv[:, nb:2 * nb], False, True))
+                m2 = mm(256, [rd, OH[hf], OH[2 + hf]], calls)
+                cv.append(ts(2 * nb, [m2], off[:, 2 * hf * nb:2 * (hf + 1) * nb], ps[:, 0:2 * nb], -float(UM + MV[3]), None, A.add, late=-300))
+            ca = min(max(2 * int(round(ACT_SHARE[i] * 2 * nb)), 2 * nb), 4 * nb)
+
+            def need(a, b):
+                return [cv[x] for x in range(2) if a < 2 * (x + 1) * nb and b > 2 * x * nb] + pyr
+
+            ga = []
+            for a in range(ca, 4 * nb, GP):
+                b = min(a + GP, 4 * nb)
+                ga.append((a, b, op("V", 50, need(a, b), lambda a=a, b=b, gt=gt, off=off, win=win:
+                                    V.tensor_copy(gt[:, 16 * a:16 * b], win[:, 0:WIN].indirect(off[:, a:b])), ge=16 * (b - a))))
+            pieces = [(max(ca, 3 * nb), 4 * nb), (ca, 3 * nb)]
+            for nh in range(4):
+                a, b = nh * nb, min((nh + 1) * nb, ca)
+                if a < b:
+                    pieces.append((a, b))
+                    ga.append((a, b, op("A", 65, need(a, b), lambda a=a, b=b, gt=gt, off=off, win=win:
+                                        S.activation(gt[:, 16 * a:16 * b], win[:, 0:WIN].indirect(off[:, a:b]), AF.Copy), ge=16 * (b - a))))
+            scs = [(a, b, v(8 * (b - a), [k for x, y, k in ga if x < b and y > a] + [iseg], lambda a=a, b=b, gt=gt, sc=sc:
+                            V.tensor_tensor_scan(sc[:, 16 * a:16 * b], T.seg[:, 0:16 * (b - a)], gt[:, 16 * a:16 * b], 0.0, A.min, A.max), -100))
+                   for a, b in pieces if a < b]
+            pz = pa[0:24, 0:nb]
+            z = mm(32, [cv[0], CZ], [(pz, T.cz[:, 0:24], src, True, False)])
+            for j, nh in enumerate([3, 0, 1, 2] if ca <= 3 * nb else [0, 1, 2, 3]):
+                calls = [(pz, wz[:, 4 * nh + n4:384:16], sc[:, 16 * nh * nb + 4 * n4 + 3:16 * (nh + 1) * nb:16], False,
+                          j == 3 and n4 == 3) for n4 in range(4)]
+                z = mm(4 * max(24, nb), [k for x, y, k in scs if x < (nh + 1) * nb and y > nh * nb] + WZ, calls, after=[z])
+            if h == N - 1:
+                alls = [k for x, y, k in scs]
+                if NCOPY:
+                    feat(i, sc, 4, alls)
+                else:
+                    fc = T["fc%d" % i]
+                    cp = v(8 * nb, alls, lambda fc=fc, sc=sc, nb=nb: V.tensor_copy(fc[:], sc[:, 3:64 * nb:4]))
+                    farr[i] = send(fc[:], T["fl%d" % i][:], peer(1), "af%d" % i, [cp], 60 * nb)
+            n1 = ts(nb, [z, m1], sb[0:24, sa:sa + nb], pz, 92160.0, 104448.0, A.max, A.min, late=-400)
+            n3 = update(src, tt[:], pb, nb, [n1, cv[1]])
+            if h == N - 1 and NCOPY:
+                hist[i] = trail(i, range(N - 1), [n1], [n3 - 1])
+            bank[i] = prev[i] = finish(mb[0:64, oa:oa + nb], mb[64:128, oa:oa + nb], tt, pa, nb, [n3] + clr, h == N - 1)
+            if STEPS[h][1]:
+                mbs[i] = T["mb%d_%d" % (h + 1, i)]
+                prev[i] = send(mb[:, 0:(h + 1) * w], mbs[i][:, 0:(h + 1) * w], peer(STEPS[h][1]), "ar%d_%d" % (h + 1, i), [bank[i]], 0)
+
+    for i, nb in enumerate(BATCH):
+        if NCOPY:
+            mt = trail(i, [N - 1], [prev[i]], [hist[i]])
+        else:
+            feat(i, T["fl%d" % i], 1, [farr[i]])
+            mt = trail(i, range(N), [prev[i], bank[i]], [])
+        to.append(act(nb, [mt], T.tr[0:96, B0[i]:B0[i] + nb], T["pa%d" % i][0:96, 0:nb]))
+    op("Y", 3000, fo, lambda: Y.dma_start(T.feat[:], T.ft[:]), sem=("dft", 16))
+    op("A", 2000, to, lambda: S.dma_start(T.trail[:], T.tr[0:96, :]), sem=("dtr", 16))
+    return ops, nsent[0]
+
+
+PLANS = []
+
+
+def rank_program(g, core, T, topo):
+    if T.rank_of(core) is None:
+        helper(g, core, T, topo)
+        return
+    ops, nsent = build(g, T, topo, core)
+    if not PLANS:
+        PLANS.append(plan(ops)[0])
+    order = PLANS[0]
+    Q = {"V": g.vector, "A": g.scalar, "P": g.tensor, "G": g, "Y": g.sync}
+    needed = set(d for o in ops for d in o["deps"])
+    sig = {}
+    count = {}
+    for k in order:
+        o = ops[k]
+        if o["sem"] is None:
+            if k in needed:
+                s = "c" + o["q"]
+                count[s] = count.get(s, 0) + 1
+                sig[k] = (s, count[s])
+        elif o["sem"]:
+            sig[k] = o["sem"]
+            count[o["sem"][0]] = max(count.get(o["sem"][0], 0), o["sem"][1])
+    seen = {}
+    drain = []
+    for k in order:
+        o = ops[k]
+        if o["q"] == "X":
+            continue
+        want = {}
+        for d in o["deps"] + (drain if o["q"] == "V" else []):
+            s, n = sig[d]
+            want[s] = max(want.get(s, 0), n)
+        for s in sorted(want):
+            if seen.get((o["q"], s), 0) < want[s]:
+                Q[o["q"]].wait_ge(T.sem[s], want[s])
+                seen[(o["q"], s)] = want[s]
+        r = o["fn"]()
+        if o["q"] == "V":
+            drain = [k] if o["drain"] else []
+        if k in sig:
+            r.then_inc(T.sem[sig[k][0]], 1 if o["sem"] is None else 16)
+    count["sent"] = nsent
+    for s in sorted(count):
+        if not any(seen.get((q, s), 0) >= count[s] for q in Q):
+            g.sync.wait_ge(T.sem[s], count[s])

@@ -4,26 +4,24 @@ from concourse.mybir import AluOpType as A, ActivationFunctionType as AF
 
 N = 4
 SIM = 112
-BATCH = [22, 22, 20]
-ACT_SHARE = [0.72, 0.72, 0.72]
-GP = 12
-NCOPY = 1
-WAYS = 2
-NCH = 8
-PLANFOR = [(1800, 1.15, 50., 90.), (3000, 1.5, 60., 110.), (2500, 1.9, 60., 110.), (4200, 1.5, 80., 160.)]
-TRIES = 20000
-STEPS = [[("win", 1), ("win", 1), ("win", 1), ("win", 1)],
-         [("win", 1), ("win", 1), ("win", -2), ("win2", 0)],
-         [("win", 1), ("win", 0), ("win3", -1), ("win2", 0)]][NCOPY]
-COPIES = [[], [(1, "win2")], [(-1, "win3"), (1, "win2")]][NCOPY]
+BATCH = [32, 32]
+ACT_SHARE = [0.7, 0.7]
+GP = 16
+NCOPY = 2
+PLANFOR = [(3000, 1.15, 50., 90.), (4000, 1.5, 60., 110.), (3500, 1.9, 60., 110.), (5000, 1.4, 80., 160.)]
+TRIES = 80000
+STEPS = [None, [("win", 1), ("win", 1), ("win", -2), ("win2", 0)], [("win", 1), ("win", 0), ("win3", -1), ("win2", 0)]][NCOPY]
+COPIES = [None, [(1, "win2")], [(-1, "win3"), (1, "win2")]][NCOPY]
 NBT = len(BATCH)
 B0 = [sum(BATCH[:i]) for i in range(NBT)]
 MV = [8256, 7168, 2176, 1984]
 LV = [(0, 4096), (4096, 1024), (5120, 256), (5376, 64)]
 WIN = MV[0] - MV[3] + 4096
-BIG0 = MV[1] - MV[3]
-CW = (WIN - BIG0) // NCH
-SMALL = MV[2] - MV[3] + 256
+CW = MV[2] - MV[3] + 256
+NCH = 13
+WAYS = 6
+CH0 = [0] + [WIN - (NCH - k) * CW for k in range(1, NCH)]
+CALLS = [[0, 1, 2, 3], [4, 5, 6, 7], [8, 9, 10, 11], [12]]
 UM = 160
 NK = 10
 KF, KF2, KM, KU0, KU1, KV0, KV1, KCZ, KLO, KW = range(NK)
@@ -52,18 +50,14 @@ for _w in ["win"] + [_c[1] for _c in COPIES]:
 for _i, _nb in enumerate(BATCH):
     SCRATCH["pa%d" % _i] = ("psum", [128, 512], "float32")
     SCRATCH["pb%d" % _i] = ("psum", [128, 512], "float32")
-    if not NCOPY:
-        SCRATCH["fc%d" % _i] = ("sbuf", [128, 16 * _nb], BF)
-        SCRATCH["fl%d" % _i] = ("sbuf", [128, 16 * _nb], BF)
-    for _h in range(N + 1):
-        SCRATCH["mb%d_%d" % (_h, _i)] = ("sbuf", [128, N * (-(-_nb // 8) * 8)], BF)
     for _h in range(N):
+        SCRATCH["mb%d_%d" % (_h, _i)] = ("sbuf", [128, N * (-(-_nb // 8) * 8)], BF)
         SCRATCH["off%d_%d" % (_h, _i)] = ("sbuf", [128, 4 * _nb], "uint16")
         for _k, _n in (("uv", 2), ("gt", 64), ("sc", 64), ("tt", 1)):
             SCRATCH["%s%d_%d" % (_k, _h, _i)] = ("sbuf", [128, _n * _nb], BF)
 SEMAPHORES = (["cP", "cV", "cA", "cG", "dpyr", "dhd", "dsxy", "dbx", "dft", "dtr", "sent"]
               + [x + c[1] for c in COPIES for x in ("small", "big")] + ["ch%d" % k for k in range(NCH)]
-              + ["ar%d_%d" % (h, i) for h in range(1, N + 1) for i in range(NBT)] + ["af%d" % i for i in range(NBT)])
+              + ["ar%d_%d" % (h, i) for h in range(1, N) for i in range(NBT)])
 CY = 1.04
 
 
@@ -120,7 +114,7 @@ def plan(ops):
     low, kept = cur, order
     for it in range(TRIES):
         end, why, res = runs[int(rnd() * len(runs))]
-        k, crit = max(range(n), key=end.index if False else (lambda x: end[x])), []
+        k, crit = end.index(max(end)), []
         while k >= 0:
             if res[k] and why[k] >= 0 and why[k] not in pre[k]:
                 crit.append(k)
@@ -151,7 +145,7 @@ def plan(ops):
             continue
         o2 = order[:pa] + new + order[pb + 1:]
         val, r2 = value(o2)
-        if val < cur or rnd() < math.exp((cur - val) / (150.0 * (1 - it / TRIES) + 5)):
+        if val < cur or rnd() < math.exp((cur - val) / (100.0 * (1 - it / TRIES) + 5)):
             order, cur, runs = o2, val, r2
             if cur < low:
                 low, kept = cur, order
@@ -160,34 +154,36 @@ def plan(ops):
 
 def routes(src, dst, c, topo):
     own = topo.cores_of(src)
-    far = [x for x in own if topo.die(x) != topo.die(src)]
-    first = [[x for x in far if topo.may_write(x, dst)][0],
-             [x for x in own if topo.die(x) == topo.die(src) and x != src][0],
-             [x for x in far if not topo.may_write(x, dst)][0]]
-    ways = [[first[0]]]
-    for b in first[1:WAYS]:
-        ways.append([b, [x for x in range(SIM) if topo.mates(topo.chip(x), topo.chip(dst)) and topo.die(x) == topo.die(b)
-                         and topo.may_write(b, x) and topo.may_write(x, dst)][c]])
-    return ways
+    far = [x for x in own if topo.die(x) != topo.die(src) and topo.may_write(x, dst)]
+    ways = [[[far[0]], [far[1]]]]
+    for same in (True, False):
+        first = [x for x in own if (topo.die(x) == topo.die(src)) == same and not topo.may_write(x, dst)]
+        relay = [x for x in range(SIM) if topo.mates(topo.chip(x), topo.chip(dst)) and topo.die(x) == topo.die(first[0])
+                 and topo.may_write(x, dst)]
+        ways.append([[first[j], relay[(c + j) % 2]] for j in range(2)])
+    return [ways[w % 3][w // 3] for w in range(WAYS)]
 
 
 def chunk(t, k):
-    return t[:, BIG0 + k * CW:BIG0 + (k + 1) * CW]
+    return t[:, CH0[k]:CH0[k] + CW]
 
 
-def first_masks(src, dst, topo, j):
+def first_engines(src, dst, topo, k):
     off = topo.engines(src, dst)
-    rest = [e for e in topo.engines(src, routes(src, dst, 0, topo)[0][0]) if e not in off]
-    sets = [rest, off] if j == 0 else [rest[:len(rest) // 2], rest[len(rest) // 2:]]
-    return [(sum(1 << e for e in s), len(s)) for s in sets]
+    every = topo.engines(src, routes(src, dst, 0, topo)[0][0])
+    j = [k in c for c in CALLS].index(True)
+    use = every if j < 2 else [e for e in every if e not in off]
+    if len(CALLS[j]) == 1:
+        return use
+    p, half = CALLS[j].index(k), len(use) // 2
+    return use[half * (p // 2):half * (p // 2 + 1)][p % 2::2]
 
 
 def helper(g, core, T, topo):
     n = 0
-    for r in range(N):
-        src = T.cores[r]
-        for c, (d, wn) in enumerate(COPIES):
-            dst = T.cores[(r + d) % N]
+    for c, (d, wn) in enumerate(COPIES):
+        for r in range(N):
+            src, dst = T.cores[r], T.cores[(r + d) % N]
             for w, way in enumerate(routes(src, dst, c, topo)):
                 if core not in way:
                     continue
@@ -196,9 +192,9 @@ def helper(g, core, T, topo):
                 rid, pid, _ = topo.addr(to)
                 for k in range(w, NCH, WAYS):
                     if p or c == 0:
-                        g.wait_ge(T.sem["ch%d" % k], len(topo.engines(way[0], core)) if p else first_masks(src, dst, topo, k // 2)[k % 2][1])
+                        g.wait_ge(T.sem["ch%d" % k], len(topo.engines(way[0], core) if p else first_engines(src, dst, topo, k)))
                     g.remote_dma(chunk(T[wn] if to == dst else T.win, k), chunk(T.win, k),
-                                 T.sem["big" + wn] if to == dst else T.sem["ch%d" % k], T.sem.sent, pid, rid, topo.mask(core, to))
+                                 T.sem[("big" if k else "small") + wn if to == dst else "ch%d" % k], T.sem.sent, pid, rid, topo.mask(core, to))
                     n += len(topo.engines(core, to))
     if n:
         g.wait_ge(T.sem.sent, n)
@@ -250,7 +246,7 @@ def build(g, T, topo, core):
     dbx = load("A", T.bx[0:24, :], T.box[:], ("dbx", 16), 2000)
     dhd = load("A", T.win[:, 64:112], T.head[:], ("dhd", 16), 2000)
     for l, (a, n) in enumerate(LV):
-        dp = load("Y", T.win[:, MV[l] - MV[3]:MV[l] - MV[3] + n], T.pyr[:, a:a + n], ("dpyr", 16 * (l + 1)), 6500)
+        dp = load("Y", T.win[:, MV[l] - MV[3]:MV[l] - MV[3] + n], T.pyr[:, a:a + n], ("dpyr", 16 * (l + 1)), 5600)
 
     zk = fill(80, T.krow[0:1, :], 0.0)
     zo = fill(64, T.zrow[0:1, 120:128], 1.0)
@@ -261,7 +257,7 @@ def build(g, T, topo, core):
         if j % 5 in (1, 3):
             ks.append(act(1, [zk, zo], ap, T.zrow[0:1, 120:120 + len(range(a, b, st))], val))
         else:
-            ks.append(fill(1, ap, val, [zk]))
+            ks.append(fill(1, ap, val, [zk], -200))
     mk = mm(1024, ks, [(T.pa0[:, 0:NK], T.zrow[0:1, 120 - 8 * t:248 - 8 * t], T.krow[0:1, t * NK:(t + 1) * NK], t == 0, t == 15)
                        for t in range(16)])
 
@@ -281,9 +277,6 @@ def build(g, T, topo, core):
     eg = T.eg
     ipi = gi(T.pi[:, 0:1], [[0, 1]], 0, 1)
     iic = gi(T.icol[:], [[1, 128]], 0, 0)
-    ig8 = gi(T.g8[:], [[0, 4], [1, 8]], 0, 0)
-    ijr = gi(T.jrow[:], [[0, 8], [1, 16]], 0, 0)
-    igr = gi(T.grow[:], [[1, 8], [0, 16]], 0, 0)
     gi(eg[64:128, 0:40], [[-1, 40]], 0, 1, 1.0, [ze])
     gi(eg[64:128, 64:128], [[0, 8], [-1, 8]], -16, 1, -1.0)
     gi(eg[0:32, 0:24], [[-1, 3], [-3, 8]], 0, 1, 1 / 512)
@@ -291,6 +284,9 @@ def build(g, T, topo, core):
     gi(eg[0:32, 64:128], [[0, 8], [-3, 8]], -2, 1, -1 / 512)
     gi(eg[64:128, 0:40], [[0, 40]], -48, 1, -192.0)
     EG = gi(eg[64:128, 64:128], [[0, 64]], -48, 1, 256.0)
+    ig8 = gi(T.g8[:], [[0, 4], [1, 8]], 0, 0)
+    ijr = gi(T.jrow[:], [[0, 8], [1, 16]], 0, 0)
+    igr = gi(T.grow[:], [[1, 8], [0, 16]], 0, 0)
     iseg = gi(T.seg[:], [[0, 4 * max(BATCH)], [256, 4]], 0, 0)
     zp = fill(64, T.pw[:], 0.0, late=2000)
     for e, o in ((0, 0), (1, 32), (2, 16)):
@@ -326,42 +322,30 @@ def build(g, T, topo, core):
         w = [act(48, [mgk, d2], wz[:, 48 * j:48 * j + 48], win[:, 64:112], T.mg[:, j:j + 1], late) for j in range(8)]
         return win, oh, wz, o, w, pyr
 
-    pyr0 = [dp, dhd, sco, fill(1, T.win[:, 120:192], 0.0), fill(1, T.win[:, 6208:6272], 0.0)]
+    pyr0 = [dp, dhd, sco] + [fill((b - a) / 2, T.win[:, a:b], 0.0) for a, b in ((120, 192), (CH0[1], MV[1] - MV[3]), (6208, 6272))]
     frames = {"win": frame("win", sco, dhd, pyr0, 0.0)}
     nsent = [0]
 
-    def send(src, dst, to, sem, deps, cost, after=()):
-        rid, pid, _ = topo.addr(to)
-        nsent[0] += len(topo.engines(core, to))
-        s = op("G", 600, deps, lambda: g.remote_dma(dst, src, T.sem[sem], T.sem.sent, pid, rid, topo.mask(core, to)), sem=(), after=after)
-        return op("X", cost, [], None, sem=(sem, len(topo.engines(core, to))), after=[s], hp=1)
+    ways = routes(core, peer(1), 0, topo)
+    last = []
+    for call in CALLS:
+        eng = [first_engines(core, peer(1), topo, k) for k in call]
 
-    if COPIES:
-        ways = routes(core, peer(1), 0, topo)
-        last = []
-        small = {}
-        for j in range(NCH // 2):
-            ms = first_masks(core, peer(1), topo, j)
-
-            def fused(j=j, ms=ms):
-                trs = []
-                for w in range(2):
-                    k = 2 * j + w
-                    rid, pid, _ = topo.addr(ways[k % WAYS][0])
-                    trs.append(RemoteDMATransfer(dst_ids=[DstId(rid=rid, pnc=pid)], dma_engine_mask=ms[w][0],
-                                                 remote_sem=T.sem["ch%d" % k], src=chunk(T.win, k), dst=chunk(T.win, k)))
-                return g.remote_dma_fused(trs, local_sem=T.sem.sent)
-            nsent[0] += ms[0][1] + ms[1][1]
-            last = [op("G", 600, pyr0, fused, sem=(), after=last)]
-            if j < len(COPIES):
-                d, wn = COPIES[j]
-                small[wn] = send(T.win[:, 0:SMALL], T[wn][:, 0:SMALL], peer(d), "small" + wn, pyr0, 2500, last)
-                last = [small[wn] - 1]
-        for c, (d, wn) in enumerate(COPIES):
-            back = routes(peer(-d), core, c, topo)
-            nbig = sum(len(topo.engines(back[k % WAYS][-1], core)) for k in range(NCH))
-            big = op("X", 9000 + 6000 * c, [], None, sem=("big" + wn, nbig), after=last)
-            frames[wn] = frame(wn, small[wn], small[wn], [small[wn], big], 400.0)
+        def fused(call=call, eng=eng):
+            trs = []
+            for k, es in zip(call, eng):
+                rid, pid, _ = topo.addr(ways[k % WAYS][0])
+                trs.append(RemoteDMATransfer(dst_ids=[DstId(rid=rid, pnc=pid)], dma_engine_mask=sum(1 << e for e in es),
+                                             remote_sem=T.sem["ch%d" % k], src=chunk(T.win, k), dst=chunk(T.win, k)))
+            return g.remote_dma_fused(trs, local_sem=T.sem.sent)
+        nsent[0] += sum(len(es) for es in eng)
+        last.append(op("G", 700, pyr0, fused, sem=(), after=last[-1:]))
+    for c, (d, wn) in enumerate(COPIES):
+        back = routes(peer(-d), core, c, topo)
+        cnt = [len(topo.engines(back[k % WAYS][-1], core)) for k in range(NCH)]
+        small = op("X", 7000 + 8000 * c, [], None, sem=("small" + wn, cnt[0]), after=last[:1])
+        big = op("X", 9500 + 7000 * c, [], None, sem=("big" + wn, sum(cnt[1:])), after=last[-1:])
+        frames[wn] = frame(wn, small, small, [small, big], 400.0)
 
     def update(src, tt, pb, nb, deps):
         mt = mm(64, deps + [EG], [(pb[:, 0:nb], eg[:], src, True, True)])
@@ -379,15 +363,7 @@ def build(g, T, topo, core):
     prev = [init] * NBT
     bank = [init] * NBT
     mbs = [T["mb0_%d" % i] for i in range(NBT)]
-    farr = [None] * NBT
-    hist = [None] * NBT
     fo, to = [], []
-
-    def feat(i, src, step, deps):
-        nb = BATCH[i]
-        for n4 in range(4):
-            o, s = T.ft[:, n4:16:4, B0[i]:B0[i] + nb], src[:, (n4 + 1) * step - 1:16 * nb * step:4 * step]
-            fo.append(act(4 * nb, deps, o, s) if n4 % 2 else v(2 * nb, deps, lambda o=o, s=s: V.tensor_copy(o, s)))
 
     def trail(i, hs, deps, after):
         nb, w = BATCH[i], -(-BATCH[i] // 8) * 8
@@ -445,28 +421,26 @@ def build(g, T, topo, core):
                 z = mm(4 * max(24, nb), [k for x, y, k in scs if x < (nh + 1) * nb and y > nh * nb] + WZ, calls, after=[z])
             if h == N - 1:
                 alls = [k for x, y, k in scs]
-                if NCOPY:
-                    feat(i, sc, 4, alls)
-                else:
-                    fc = T["fc%d" % i]
-                    cp = v(8 * nb, alls, lambda fc=fc, sc=sc, nb=nb: V.tensor_copy(fc[:], sc[:, 3:64 * nb:4]))
-                    farr[i] = send(fc[:], T["fl%d" % i][:], peer(1), "af%d" % i, [cp], 60 * nb)
+                for n4 in range(4):
+                    o, s = T.ft[:, n4:16:4, B0[i]:B0[i] + nb], sc[:, 4 * n4 + 3:64 * nb:16]
+                    fo.append(act(4 * nb, alls, o, s) if n4 % 2 else v(2 * nb, alls, lambda o=o, s=s: V.tensor_copy(o, s)))
             n1 = ts(nb, [z, m1], sb[0:24, sa:sa + nb], pz, 92160.0, 104448.0, A.max, A.min, late=-400)
             n3 = update(src, tt[:], pb, nb, [n1, cv[1]])
-            if h == N - 1 and NCOPY:
-                hist[i] = trail(i, range(N - 1), [n1], [n3 - 1])
+            if h == N - 1:
+                hist = trail(i, range(N - 1), [n1], [n3 - 1])
             bank[i] = prev[i] = finish(mb[0:64, oa:oa + nb], mb[64:128, oa:oa + nb], tt, pa, nb, [n3] + clr, h == N - 1)
+            if h == N - 1:
+                to.append(act(nb, [trail(i, [h], [prev[i]], [hist])], T.tr[0:96, B0[i]:B0[i] + nb], pa[0:96, 0:nb]))
             if STEPS[h][1]:
                 mbs[i] = T["mb%d_%d" % (h + 1, i)]
-                prev[i] = send(mb[:, 0:(h + 1) * w], mbs[i][:, 0:(h + 1) * w], peer(STEPS[h][1]), "ar%d_%d" % (h + 1, i), [bank[i]], 0)
+                dst, sem = peer(STEPS[h][1]), "ar%d_%d" % (h + 1, i)
+                ne = len(topo.engines(core, dst))
+                nsent[0] += ne
+                s = op("G", 600, [bank[i]], lambda a=mbs[i][:, 0:oa + w], b=mb[:, 0:oa + w], dst=dst, sem=sem:
+                       g.remote_dma(a, b, T.sem[sem], T.sem.sent, topo.addr(dst)[1], topo.addr(dst)[0], topo.mask(core, dst)),
+                       sem=(), after=last[-1:] + [PW])
+                prev[i] = op("X", 0, [], None, sem=(sem, ne), after=[s], hp=1)
 
-    for i, nb in enumerate(BATCH):
-        if NCOPY:
-            mt = trail(i, [N - 1], [prev[i]], [hist[i]])
-        else:
-            feat(i, T["fl%d" % i], 1, [farr[i]])
-            mt = trail(i, range(N), [prev[i], bank[i]], [])
-        to.append(act(nb, [mt], T.tr[0:96, B0[i]:B0[i] + nb], T["pa%d" % i][0:96, 0:nb]))
     op("Y", 3000, fo, lambda: Y.dma_start(T.feat[:], T.ft[:]), sem=("dft", 16))
     op("A", 2000, to, lambda: S.dma_start(T.trail[:], T.tr[0:96, :]), sem=("dtr", 16))
     return ops, nsent[0]

@@ -4,60 +4,67 @@ from concourse.mybir import AluOpType as A, ActivationFunctionType as AF
 
 N = 4
 SIM = 112
-BATCH = [32, 32]
-ACT_SHARE = [0.7, 0.7]
-GP = 16
-NCOPY = 2
-PLANFOR = [(3000, 1.15, 50., 90.), (4000, 1.5, 60., 110.), (3500, 1.9, 60., 110.), (5000, 1.4, 80., 160.)]
-TRIES = 80000
-STEPS = [None, [("win", 1), ("win", 1), ("win", -2), ("win2", 0)], [("win", 1), ("win", 0), ("win3", -1), ("win2", 0)]][NCOPY]
-COPIES = [None, [(1, "win2")], [(-1, "win3"), (1, "win2")]][NCOPY]
+BATCH = [22, 22, 20]
+VSHARE = [0.22] * 4
+SPLIT = False
+CUTS = [2, 3, 4]
+SEG = 16 * max(BATCH) * max(b - a for a, b in zip([0] + CUTS, CUTS))
+PLANFOR = [(3000, 1.2, 50., 90.), (4000, 1.56, 70., 130.), (3500, 1.9, 60., 110.), (5000, 1.4, 120., 220.)]
+STARTS, TRIES = 200, 60000
+EARLY = 4.5
+LOADED = [3000, 4000, 5200, 6400]
+ARRIVE = [4500, 9500, 14500]
+STEPS = ["win", "win1", "win2", "win3"]
+COPIES = [(-h, STEPS[h]) for h in range(1, N)]
 NBT = len(BATCH)
 B0 = [sum(BATCH[:i]) for i in range(NBT)]
 MV = [8256, 7168, 2176, 1984]
 LV = [(0, 4096), (4096, 1024), (5120, 256), (5376, 64)]
 WIN = MV[0] - MV[3] + 4096
-CW = MV[2] - MV[3] + 256
-NCH = 13
-WAYS = 6
-CH0 = [0] + [WIN - (NCH - k) * CW for k in range(1, NCH)]
-CALLS = [[0, 1, 2, 3], [4, 5, 6, 7], [8, 9, 10, 11], [12]]
+SMALL = MV[2] - MV[3] + 256
+WAYS, SUB = 7, 2
+CW = 372
+BIG = WIN - WAYS * SUB * CW
+CALLS = [(s, ws) for s in range(SUB) for ws in ((0, 1, 2, 3), (4, 5, 6))]
 UM = 160
-NK = 10
-KF, KF2, KM, KU0, KU1, KV0, KV1, KCZ, KLO, KW = range(NK)
-KTAB = [(KF, 13, 14, 1, 0.5), (KF, 14, 15, 1, 0.25), (KF, 7, 16, 8, 0.125), (KF, 6, 7, 1, -38.0),
-        (KF2, 13, 14, 1, 0.75), (KF2, 14, 15, 1, 0.1875), (KF2, 15, 16, 1, 3 / 64), (KF2, 6, 7, 1, -47.25),
-        (KF2, 7, 8, 1, 1 / 64),
-        (KM, 13, 14, 1, 1088.0), (KM, 14, 15, 1, 4992.0), (KM, 15, 16, 1, 192.0), (KM, 6, 7, 1, -257024.0),
-        (KM, 7, 8, 1, -320.0),
-        (KU0, 0, 1, 1, 1.0), (KU0, 14, 15, 1, float(UM)), (KU0, 15, 16, 1, -127 / 256), (KU1, 2, 3, 1, 1 / 16),
-        (KV0, 4, 5, 1, 64.0), (KV0, 1, 2, 1, -31.75), (KV0, 5, 6, 1, 1.0), (KV1, 3, 4, 1, 4.0),
-        (KLO, 1, 10, 4, 1.0), (KLO, 6, 8, 1, 1.0), (KLO, 2, 4, 1, 4.0), (KLO, 8, 13, 4, 8.0), (KLO, 10, 12, 1, 56.0),
-        (KLO, 13, 14, 1, 52.0), (KLO, 14, 15, 1, 40.0), (KLO, 15, 16, 1, 16.0),
-        (KW, 0, 5, 1, 64.0), (KW, 8, 13, 4, 52.0), (KW, 13, 16, 1, 1.0),
-        (KCZ, 13, 14, 1, 12288.0), (KCZ, 14, 15, 1, -32.0), (KCZ, 15, 16, 1, 1 / 16)]
+NK = 15
+KF, KF2, KM, KU0, KU1, KV0, KV1, KCZ, KUP, KL1, KL2, KX, KY, KS, KC = range(NK)
+KTAB = [(KF, 5, 1, 1, 0.5), (KF, 6, 1, 1, 0.25), (KF, 7, 2, 7 * NK, 0.125), (KF, 13, 1, 1, -38.0),
+        (KF2, 5, 1, 1, 0.75), (KF2, 6, 1, 1, 0.1875), (KF2, 7, 1, 1, 3 / 64), (KF2, 13, 1, 1, -47.25), (KF2, 14, 1, 1, 1 / 64),
+        (KM, 5, 1, 1, 1088.0), (KM, 6, 1, 1, 4992.0), (KM, 7, 1, 1, 192.0), (KM, 13, 1, 1, -257024.0), (KM, 14, 1, 1, -320.0),
+        (KU0, 0, 1, 1, 1.0), (KU0, 14, 1, 1, float(UM)), (KU0, 15, 1, 1, -127 / 256), (KU1, 2, 1, 1, 1 / 16),
+        (KV0, 4, 1, 1, 64.0), (KV0, 1, 1, 1, -31.75), (KV0, 5, 1, 1, 1.0), (KV1, 3, 1, 1, 4.0),
+        (KCZ, 13, 1, 1, 12288.0), (KCZ, 14, 1, 1, -32.0), (KCZ, 15, 1, 1, 1 / 16),
+        (KUP, 5, 1, 1, 53.0), (KUP, 6, 1, 1, 41.0), (KUP, 7, 1, 1, 17.0), (KUP, 8, 2, 4 * NK, 60.0), (KUP, 10, 2, NK, 56.0),
+        (KL1, 5, 2, 1, 52.0), (KL1, 6, 2, 1, 40.0), (KL1, 7, 2, 1, 16.0), (KL1, 8, 2, 4 * NK, 8.0),
+        (KL1, 10, 2, 1, 4.0), (KL1, 11, 2, 1, 4.0),
+        (KUP, 9, 3, 1, 1.0), (KUP, 13, 3, 1, 1.0), (KUP, 14, 3, 1, 1.0), (KUP, 15, 3, 1, 1.0),
+        (KX, 0, 3, NK + 1, 1 / 512), (KX, 14, 3, 1, -192.0), (KX, 8, 2, 2 * NK + 2, 1.0), (KY, 12, 1, 1, 1.0),
+        (KC, 2, 1, 1, -1 / 512), (KC, 10, 1, 1, -1.0), (KC, 14, 1, 1, 256.0)]
+NEWS = [[(0, 80, KC), (80, 96, KS), (96, 128, KC)], [(0, 64, KC), (64, 80, KX), (80, 96, KS), (96, 128, KY)]]
 
 BF = "bfloat16"
 SCRATCH = {"sxy": ("sbuf", [128, 16], "int32"), "bx": ("sbuf", [128, 64], "int32"), "pi": ("sbuf", [128, 4], "int32"),
            "kc": ("sbuf", [128, 16], "float32"), "pf": ("sbuf", [128, 4], "float32"), "mg": ("sbuf", [128, 8], "float32"),
            "tr": ("sbuf", [128, 64], "float32"), "ft": ("sbuf", [128, 16, 64], BF)}
-for _k, _n in dict(krow=16 * NK, zrow=256, icol=128, jrow=128, grow=128, g8=32, mkl=128, tmpl=256, l1=256, fm=64, cz=32, eg=128,
-                   pw=112, seg=16 * max(BATCH), i0=64, i1=64, ti=64).items():
+for _k, _n in dict(krow=16 * NK, zrow=256, icol=128, jrow=128, grow=128, g8=80, mkl=128, tmpl=256, l1=256, fm=64, cz=32,
+                   eg=256, pw=112, seg=SEG, i0=64, i1=192, lim=192).items():
     SCRATCH[_k] = ("sbuf", [128, _n], BF)
 for _w in ["win"] + [_c[1] for _c in COPIES]:
-    for _k, _n in (("", WIN), ("wz", 384), ("ot", 1024), ("oh", 1024)):
+    SCRATCH["wz" + _w] = ("sbuf", [128, 3, 128], BF)
+    for _k, _n in (("", WIN), ("ot", 1024), ("oh", 1024)):
         SCRATCH[_k + _w] = ("sbuf", [128, _n], BF)
 for _i, _nb in enumerate(BATCH):
     SCRATCH["pa%d" % _i] = ("psum", [128, 512], "float32")
     SCRATCH["pb%d" % _i] = ("psum", [128, 512], "float32")
+    SCRATCH["mb%d" % _i] = ("sbuf", [128, N * 3 * _nb], BF)
     for _h in range(N):
-        SCRATCH["mb%d_%d" % (_h, _i)] = ("sbuf", [128, N * (-(-_nb // 8) * 8)], BF)
         SCRATCH["off%d_%d" % (_h, _i)] = ("sbuf", [128, 4 * _nb], "uint16")
-        for _k, _n in (("uv", 2), ("gt", 64), ("sc", 64), ("tt", 1)):
+        for _k, _n in (("uv", 2), ("gt", 64), ("sc", 64)):
             SCRATCH["%s%d_%d" % (_k, _h, _i)] = ("sbuf", [128, _n * _nb], BF)
-SEMAPHORES = (["cP", "cV", "cA", "cG", "dpyr", "dhd", "dsxy", "dbx", "dft", "dtr", "sent"]
-              + [x + c[1] for c in COPIES for x in ("small", "big")] + ["ch%d" % k for k in range(NCH)]
-              + ["ar%d_%d" % (h, i) for h in range(1, N) for i in range(NBT)])
+SEMAPHORES = (["cP", "cV", "cA", "cG", "dp0", "dhd", "dsxy", "dbx", "dft", "dtr", "sent"] + ["dw" + w for w in STEPS[1:]]
+              + [x + c[1] for c in COPIES for x in ("small", "big")] + ["ch%d" % s for s in range(SUB)]
+              + ["dp%d" % (j + 1) for j in range(len(CALLS))] + ["rl%d_%d" % (c, s) for c in range(N - 1) for s in range(SUB)])
 CY = 1.04
 
 
@@ -68,6 +75,7 @@ def plan(ops):
     cases = [([[(d, l1 if q[d] == q[k] else l2) for d in o["deps"]] + [(d, 0.) for d in o["after"]] for k, o in enumerate(ops)],
               [o["cost"] + o["ge"] * gc * CY + o["hp"] * hop for o in ops]) for hop, gc, l1, l2 in PLANFOR]
     tail = [o["tail"] for o in ops]
+    urge = [k for k, o in enumerate(ops) if o["sem"] == ()][:1 + len(CALLS)]
 
     def replay(order, case):
         dep, cost = case
@@ -83,23 +91,6 @@ def plan(ops):
                 free[e], last[e] = end[k] - tail[k], k
         return end, why, res
 
-    dep, cost = cases[1]
-    end, free, order, todo = {}, [0.] * 6, [], list(range(n))
-    while todo:
-        best = None
-        for k in todo:
-            if all(d in end for d in pre[k]):
-                t = max([free[q[k]]] + [end[d] + l for d, l in dep[k]])
-                key = (t + ops[k]["late"], k)
-                if best is None or key < best[0]:
-                    best = (key, k, t)
-        _, k, t = best
-        end[k] = t + cost[k]
-        if q[k] != 5:
-            free[q[k]] = end[k] - tail[k]
-        order.append(k)
-        todo.remove(k)
-
     seed = [12345]
 
     def rnd():
@@ -108,8 +99,42 @@ def plan(ops):
 
     def value(o):
         r = [replay(o, c) for c in cases]
-        return sum(max(x[0]) for x in r) / len(r), r
+        return sum(max(x[0]) + sum(0.2 * x[0][k] for k in urge) for x in r) / len(r), r
 
+    suc = [[] for _ in ops]
+    for k in range(n):
+        for d in pre[k]:
+            suc[d].append(k)
+    first = None
+    for it in range(STARTS):
+        dep, cost = cases[it % len(cases)]
+        rest = [0.] * n
+        for k in reversed(range(n)):
+            rest[k] += cost[k]
+            for d, l in dep[k]:
+                rest[d] = max(rest[d], rest[k] + l)
+        win, noise = (0, 50, 100, 200)[int(rnd() * 4)], (0, 100, 300)[int(rnd() * 3)]
+        pri = [1e9 - k if tail[k] else 0.2 * rest[k] + noise * rnd() - 1e5 * ops[k]["turn"] for k in range(n)]
+        left = [len(p) for p in pre]
+        ready = {k: 0. for k in range(n) if not left[k]}
+        end, free, o = [0.] * n, [0.] * 6, []
+        while ready:
+            st = {k: max(t, free[q[k]]) for k, t in ready.items()}
+            k0 = min(st, key=st.get)
+            k = max((x for x in st if q[x] == q[k0] and st[x] <= st[k0] + win), key=lambda x: pri[x])
+            end[k] = st[k] + cost[k]
+            if q[k] != 5:
+                free[q[k]] = end[k] - tail[k]
+            o.append(k)
+            del ready[k]
+            for s in suc[k]:
+                left[s] -= 1
+                if not left[s]:
+                    ready[s] = max(end[d] + l for d, l in dep[s])
+        val = value(o)[0]
+        if first is None or val < first[0]:
+            first = (val, o)
+    order = first[1]
     cur, runs = value(order)
     low, kept = cur, order
     for it in range(TRIES):
@@ -152,31 +177,57 @@ def plan(ops):
     return kept, [max(replay(kept, c)[0]) for c in cases], replay(kept, cases[1])[0]
 
 
-def routes(src, dst, c, topo):
-    own = topo.cores_of(src)
-    far = [x for x in own if topo.die(x) != topo.die(src) and topo.may_write(x, dst)]
-    ways = [[[far[0]], [far[1]]]]
-    for same in (True, False):
-        first = [x for x in own if (topo.die(x) == topo.die(src)) == same and not topo.may_write(x, dst)]
-        relay = [x for x in range(SIM) if topo.mates(topo.chip(x), topo.chip(dst)) and topo.die(x) == topo.die(first[0])
-                 and topo.may_write(x, dst)]
-        ways.append([[first[j], relay[(c + j) % 2]] for j in range(2)])
-    return [ways[w % 3][w // 3] for w in range(WAYS)]
+def holders(src, T, topo):
+    other = T.cores[(T.rank_of(src) + 1) % N]
+    own = [x for x in topo.cores_of(src) if x != src]
+
+    def pick(near, port):
+        return [x for x in own if (topo.die(x) == topo.die(src)) == near and topo.may_write(x, other) == port]
+    a, b = pick(True, False), pick(False, False)
+    return pick(True, True)[0], [a[0], b[0], a[1], b[1]] + pick(False, True) + [src]
 
 
-def chunk(t, k):
-    return t[:, CH0[k]:CH0[k] + CW]
+def relay(w, src, dst, T, topo):
+    x = holders(src, T, topo)[1][w]
+    port = topo.may_write(x, T.cores[(T.rank_of(src) + 1) % N])
+    if port != topo.same_plane(topo.chip(src), topo.chip(dst)):
+        return None
+    on = [y for y in range(SIM) if topo.mates(topo.chip(y), topo.chip(dst)) and topo.die(y) == topo.die(x) and topo.may_write(y, dst)]
+    return on[(0, 0, 1, 1, 0, 1, 0)[w]]
 
 
-def first_engines(src, dst, topo, k):
-    off = topo.engines(src, dst)
-    every = topo.engines(src, routes(src, dst, 0, topo)[0][0])
-    j = [k in c for c in CALLS].index(True)
-    use = every if j < 2 else [e for e in every if e not in off]
-    if len(CALLS[j]) == 1:
-        return use
-    p, half = CALLS[j].index(k), len(use) // 2
-    return use[half * (p // 2):half * (p // 2 + 1)][p % 2::2]
+def piece(t, s, w):
+    a = BIG + (s * WAYS + w) * CW
+    return t[:, a:a + CW]
+
+
+def rounds(c):
+    return [[s] for s in range(SUB)]
+
+
+def transfer(T, topo, to, eng, sem, src, dst):
+    rid, pid, _ = topo.addr(to)
+    return RemoteDMATransfer(dst_ids=[DstId(rid=rid, pnc=pid)], dma_engine_mask=sum(1 << e for e in eng), remote_sem=T.sem[sem],
+                             src=src, dst=dst)
+
+
+def onward(T, topo, core, src, c, w, j, via):
+    d, wn = COPIES[c]
+    dst = T.cores[(T.rank_of(src) + d) % N]
+    r = relay(w, src, dst, T, topo) if via else None
+    to, sem = (dst, "big" + wn) if r is None else (r, "rl%d_%d" % (c, j))
+    eng, ss = topo.engines(core, to), rounds(c)[j]
+    return [transfer(T, topo, to, eng[i::len(ss)], sem, piece(T.win if via else T[wn], s, w), piece(T[wn], s, w)) for i, s in enumerate(ss)]
+
+
+def call_engines(src, T, topo, ws):
+    first, hold = holders(src, T, topo)
+    every, off = topo.engines(src, first), topo.engines(src, T.cores[(T.rank_of(src) + 1) % N])
+    if src not in [hold[w] for w in ws]:
+        half = len(every) // 2
+        return [every[half * (p // 2):half * (p // 2 + 1)][1 - p % 2::2] for p in range(len(ws))]
+    rest = [e for e in every if e not in off]
+    return [off if hold[w] == src else rest[p::2] for p, w in enumerate(ws)]
 
 
 def helper(g, core, T, topo):
@@ -184,18 +235,33 @@ def helper(g, core, T, topo):
     for c, (d, wn) in enumerate(COPIES):
         for r in range(N):
             src, dst = T.cores[r], T.cores[(r + d) % N]
-            for w, way in enumerate(routes(src, dst, c, topo)):
-                if core not in way:
+            first, hold = holders(src, T, topo)
+            ne = len(topo.engines(src, dst))
+            if core == first:
+                if c == 0:
+                    g.wait_ge(T.sem.ch0, len(topo.engines(src, core)))
+                g.remote_dma_fused([transfer(T, topo, dst, topo.engines(core, dst), "small" + wn, T.win[:, 0:SMALL], T[wn][:, 0:SMALL])],
+                                   local_sem=T.sem.sent)
+                n += ne
+    for c, (d, wn) in enumerate(COPIES):
+        for r in range(N):
+            src, dst = T.cores[r], T.cores[(r + d) % N]
+            first, hold = holders(src, T, topo)
+            for w in range(WAYS):
+                via = core == (first if c and hold[w] == src else hold[w])
+                if not via and core != relay(w, src, dst, T, topo):
                     continue
-                p = way.index(core)
-                to = way[p + 1] if p + 1 < len(way) else dst
-                rid, pid, _ = topo.addr(to)
-                for k in range(w, NCH, WAYS):
-                    if p or c == 0:
-                        g.wait_ge(T.sem["ch%d" % k], len(topo.engines(way[0], core) if p else first_engines(src, dst, topo, k)))
-                    g.remote_dma(chunk(T[wn] if to == dst else T.win, k), chunk(T.win, k),
-                                 T.sem[("big" if k else "small") + wn if to == dst else "ch%d" % k], T.sem.sent, pid, rid, topo.mask(core, to))
-                    n += len(topo.engines(core, to))
+                for j in range(len(rounds(c))):
+                    if not via:
+                        g.wait_ge(T.sem["rl%d_%d" % (c, j)], ne)
+                    elif core == first:
+                        if c == 1 and j == 0:
+                            g.wait_ge(T.sem.ch1, len(topo.engines(src, core)))
+                    elif c == 0:
+                        ws = [x for s, x in CALLS if w in x][0]
+                        g.wait_ge(T.sem["ch%d" % j], len(call_engines(src, T, topo, ws)[ws.index(w)]))
+                    g.remote_dma_fused(onward(T, topo, core, src, c, w, j, via), local_sem=T.sem.sent)
+                    n += ne
     if n:
         g.wait_ge(T.sem.sent, n)
 
@@ -203,6 +269,7 @@ def helper(g, core, T, topo):
 def build(g, T, topo, core):
     V, S, P, Y = g.vector, g.scalar, g.tensor, g.sync
     ops = []
+    turn = [-NBT - 1]
     rank = T.rank_of(core)
 
     def peer(d):
@@ -210,7 +277,7 @@ def build(g, T, topo, core):
 
     def op(q, cost, deps, fn, late=0.0, sem=None, after=(), tail=0.0, ge=0, hp=0, drain=False):
         ops.append(dict(q=q, cost=float(cost), deps=list(deps), fn=fn, late=late, sem=sem, after=list(after), tail=tail,
-                        ge=ge, hp=hp, drain=drain))
+                        ge=ge, hp=hp, drain=drain, turn=turn[0]))
         return len(ops) - 1
 
     def v(n, deps, fn, late=0.0):
@@ -243,19 +310,29 @@ def build(g, T, topo, core):
 
     load("A", T.sxy[:, 0:4], T.sx[:], ("dsxy", 16), 2000)
     dsy = load("A", T.sxy[:, 4:8], T.sy[:], ("dsxy", 32), 2000)
-    dbx = load("A", T.bx[0:24, :], T.box[:], ("dbx", 16), 2000)
     dhd = load("A", T.win[:, 64:112], T.head[:], ("dhd", 16), 2000)
-    for l, (a, n) in enumerate(LV):
-        dp = load("Y", T.win[:, MV[l] - MV[3]:MV[l] - MV[3] + n], T.pyr[:, a:a + n], ("dpyr", 16 * (l + 1)), 5600)
+    for e in range(3):
+        dbx = load("A", T.bx[8 * e:8 * e + 8, :], T.box[:, 64 * e:64 * e + 64], ("dbx", 16 * (e + 1)), 2000)
+    for j, l in enumerate((3, 2)):
+        dp0 = load("Y", T.win[:, MV[l] - MV[3]:MV[l] - MV[3] + LV[l][1]], T.pyr[:, LV[l][0]:LV[l][0] + LV[l][1]], ("dp0", 16 * (j + 1)), 2200)
+    dps = []
+    for j, (s, ws) in enumerate(CALLS):
+        lo, hi, n = BIG + (s * WAYS + ws[0]) * CW, BIG + (s * WAYS + ws[-1] + 1) * CW, 0
+        for l in (1, 0):
+            a, b = max(lo, MV[l] - MV[3]), min(hi, MV[l] - MV[3] + LV[l][1])
+            if a < b:
+                n += 1
+                o = LV[l][0] - MV[l] + MV[3]
+                dp = load("Y", T.win[:, a:b], T.pyr[:, a + o:b + o], ("dp%d" % (j + 1), 16 * n), LOADED[j])
+        dps.append(dp)
 
-    zk = fill(80, T.krow[0:1, :], 0.0)
-    zo = fill(64, T.zrow[0:1, 120:128], 1.0)
-    ze = fill(64, T.eg[:], 0.0)
+    zk = fill(8 * NK, T.krow[0:1, :], 0.0, late=-600)
+    zo = fill(64, T.zrow[0:1, 120:128], 1.0, late=-600)
     ks = [zo, fill(64, T.zrow[0:1, 0:120], 0.0), fill(64, T.zrow[0:1, 128:256], 0.0)]
-    for j, (k, a, b, st, val) in enumerate(KTAB):
-        ap = T.krow[0:1, a * NK + k:(b - 1) * NK + k + 1:st * NK]
-        if j % 5 in (1, 3):
-            ks.append(act(1, [zk, zo], ap, T.zrow[0:1, 120:120 + len(range(a, b, st))], val))
+    for j, (k, a, n, st, val) in enumerate(KTAB):
+        ap = T.krow[0:1, a * NK + k:a * NK + k + (n - 1) * st + 1:st]
+        if j % 2:
+            ks.append(act(1, [zk, zo], ap, T.zrow[0:1, 120:120 + n], val))
         else:
             ks.append(fill(1, ap, val, [zk], -200))
     mk = mm(1024, ks, [(T.pa0[:, 0:NK], T.zrow[0:1, 120 - 8 * t:248 - 8 * t], T.krow[0:1, t * NK:(t + 1) * NK], t == 0, t == 15)
@@ -263,7 +340,7 @@ def build(g, T, topo, core):
 
     lastg = []
 
-    def gi(ap, pat, base, cm, val=None, deps=()):
+    def gi(ap, pat, base, cm, val=None, deps=(), after=()):
         n = math.prod(c for _, c in pat)
         if val is None:
             def fn():
@@ -271,26 +348,16 @@ def build(g, T, topo, core):
         else:
             def fn():
                 return g.affine_select(ap, ap, pat, A.not_equal, val, base, cm)
-        lastg[:] = [op("G", 150 + 2 * n * CY, list(deps) + lastg, fn)]
+        lastg[:] = [op("G", 150 + 2 * n * CY, list(deps) + lastg, fn, after=after)]
         return lastg[0]
 
     eg = T.eg
     ipi = gi(T.pi[:, 0:1], [[0, 1]], 0, 1)
     iic = gi(T.icol[:], [[1, 128]], 0, 0)
-    gi(eg[64:128, 0:40], [[-1, 40]], 0, 1, 1.0, [ze])
-    gi(eg[64:128, 64:128], [[0, 8], [-1, 8]], -16, 1, -1.0)
-    gi(eg[0:32, 0:24], [[-1, 3], [-3, 8]], 0, 1, 1 / 512)
-    gi(eg[0:32, 24:40], [[1, 2], [-3, 8]], -2, 1, 1 / 512)
-    gi(eg[0:32, 64:128], [[0, 8], [-3, 8]], -2, 1, -1 / 512)
-    gi(eg[64:128, 0:40], [[0, 40]], -48, 1, -192.0)
-    EG = gi(eg[64:128, 64:128], [[0, 64]], -48, 1, 256.0)
-    ig8 = gi(T.g8[:], [[0, 4], [1, 8]], 0, 0)
+    ig8 = gi(T.g8[:], [[0, 10], [1, 8]], 0, 0)
     ijr = gi(T.jrow[:], [[0, 8], [1, 16]], 0, 0)
     igr = gi(T.grow[:], [[1, 8], [0, 16]], 0, 0)
-    iseg = gi(T.seg[:], [[0, 4 * max(BATCH)], [256, 4]], 0, 0)
-    zp = fill(64, T.pw[:], 0.0, late=2000)
-    for e, o in ((0, 0), (1, 32), (2, 16)):
-        PW = gi(T.pw[64:128, 9 + e:105:12], [[-1, 8]], -o, 1, 1.0, [zp])
+    iseg = fill(SEG / 8, T.seg[:, 0:SEG:4], 0.0, [fill(SEG / 2, T.seg[:], 256.0, late=1000)], 1000)
 
     p1 = ts(1, [ipi], T.pi[:, 1:2], T.pi[:, 0:1], 7, None, A.bitwise_and)
     p2 = ts(1, [ipi], T.pi[:, 2:3], T.pi[:, 0:1], 112, None, A.bitwise_and)
@@ -298,11 +365,14 @@ def build(g, T, topo, core):
     pm8, p16 = T.pf[:, 1:2], T.pf[:, 2:3]
     oi = fill(64, T.i0[:], 1.0)
     kcp = v(64, [mk], lambda: V.tensor_copy(kc[:, 0:NK], T.pa0[:, 0:NK]), -500)
-    khi = ts(1, [kcp], col(NK), col(KLO), col(KW), None, A.add, late=-500)
+    LIM = [ts(1, [kcp, iic], T.lim[:, t:192:3], T.icol[:, 0:64], 0.0, col(KUP + t), A.mult, A.add) for t in range(3)]
+    ZB = [fill(64, T["pb%d" % i][:, 256:448:3], 0.0) for i in range(NBT)]
     d0 = ts(64, [dbx, oi], T.i0[0:24, :], T.bx[0:24, :], 191.0, 512.0, A.add, A.mult, late=-500)
     FM = [ts(1, [kcp, p3, ig8], T.fm[:, a:b], T.g8[:, 0:b - a], pm8, col(k), A.is_equal, A.mult)
           for a, b, k in ((0, 24, KF), (24, 40, KF2), (40, 48, KM))]
     FM.append(fill(1, T.fm[:, 48:64], 0.0))
+    EG = [ts(1, [kcp, p3, ig8], eg[:, 128 * t + a:128 * t + b], T.g8[:, 0:b - a], pm8, col(k), A.is_equal, A.mult, late=-500)
+          for t in range(2) for a, b, k in NEWS[t]]
     ml = ts(64, [p3, igr], T.mkl[:], T.grow[:], pm8, None, A.is_equal)
     L1 = []
     for j, (k0, k1) in enumerate(((KU0, KU1), (KV0, KV1))):
@@ -319,127 +389,117 @@ def build(g, T, topo, core):
                for j in range(8)]
         o = [v(128, ots[2 * j:2 * j + 2], lambda j=j: V.transpose(oh[:, 256 * j:256 * j + 256], ot[:, 256 * j:256 * j + 256]), late)
              for j in range(4)]
-        w = [act(48, [mgk, d2], wz[:, 48 * j:48 * j + 48], win[:, 64:112], T.mg[:, j:j + 1], late) for j in range(8)]
-        return win, oh, wz, o, w, pyr
+        if wn == STEPS[0]:
+            return win, oh, wz, o, [act(48, [mgk, d2], wz[:, :, 16 * j:16 * j + 16], win[:, 64:112], T.mg[:, j:j + 1]) for j in range(8)], pyr
+        zero = act(384, [iseg], wz[:], T.seg[:, 0:384], 0.0)
+        for j in range(8):
+            w = op("Y", 2000, [zero, d2], lambda j=j: Y.dma_start(wz[16 * j:16 * j + 16, :, 16 * j:16 * j + 16], win[16 * j:16 * j + 16, 64:112]),
+                   sem=("dw" + wn, 16 * (j + 1)), tail=1900)
+        return win, oh, wz, o, [w], pyr
 
-    pyr0 = [dp, dhd, sco] + [fill((b - a) / 2, T.win[:, a:b], 0.0) for a, b in ((120, 192), (CH0[1], MV[1] - MV[3]), (6208, 6272))]
-    frames = {"win": frame("win", sco, dhd, pyr0, 0.0)}
+    gaps = [fill((b - a) / 2, T.win[:, a:b], 0.0, late=-300)
+            for a, b in ((120, 192), (BIG, MV[1] - MV[3]), (MV[1] - MV[3] + LV[1][1], MV[0] - MV[3]))]
+    frames = {"win": frame("win", sco, dhd, [dp0, dhd, sco] + gaps + dps, 0.0)}
     nsent = [0]
 
-    ways = routes(core, peer(1), 0, topo)
-    last = []
-    for call in CALLS:
-        eng = [first_engines(core, peer(1), topo, k) for k in call]
+    first, hold = holders(core, T, topo)
 
-        def fused(call=call, eng=eng):
-            trs = []
-            for k, es in zip(call, eng):
-                rid, pid, _ = topo.addr(ways[k % WAYS][0])
-                trs.append(RemoteDMATransfer(dst_ids=[DstId(rid=rid, pnc=pid)], dma_engine_mask=sum(1 << e for e in es),
-                                             remote_sem=T.sem["ch%d" % k], src=chunk(T.win, k), dst=chunk(T.win, k)))
-            return g.remote_dma_fused(trs, local_sem=T.sem.sent)
-        nsent[0] += sum(len(es) for es in eng)
-        last.append(op("G", 700, pyr0, fused, sem=(), after=last[-1:]))
+    def send(trs, n, deps, after):
+        nsent[0] += n
+        return op("G", 700, deps, lambda: g.remote_dma_fused(trs(), local_sem=T.sem.sent), -1e4, sem=(), after=after)
+
+    every, ne = topo.engines(core, first), len(topo.engines(core, peer(1)))
+    last = [send(lambda: [transfer(T, topo, first, every, "ch0", T.win[:, 0:SMALL], T.win[:, 0:SMALL])], len(every),
+                 [dp0, dhd, sco, gaps[0]], [igr])]
+    for j, (s, ws) in enumerate(CALLS):
+        def trs(s=s, ws=ws):
+            out = []
+            for w, es in zip(ws, call_engines(core, T, topo, ws)):
+                if hold[w] == core:
+                    out += onward(T, topo, core, core, 0, w, s, True)
+                else:
+                    out.append(transfer(T, topo, hold[w], es, "ch%d" % s, piece(T.win, s, w), piece(T.win, s, w)))
+            return out
+        last.append(send(trs, len(every), [dps[j]] + gaps[1:], last[-1:]))
+    own = hold.index(core)
+    later = send(lambda: [transfer(T, topo, first, every[s::SUB], "ch1", piece(T.win, s, own), piece(T.win, s, own)) for s in range(SUB)],
+                 len(every), [], last[-1:])
     for c, (d, wn) in enumerate(COPIES):
-        back = routes(peer(-d), core, c, topo)
-        cnt = [len(topo.engines(back[k % WAYS][-1], core)) for k in range(NCH)]
-        small = op("X", 7000 + 8000 * c, [], None, sem=("small" + wn, cnt[0]), after=last[:1])
-        big = op("X", 9500 + 7000 * c, [], None, sem=("big" + wn, sum(cnt[1:])), after=last[-1:])
+        small = op("X", 6500 + 5000 * c, [], None, sem=("small" + wn, ne), after=last[:1])
+        big = op("X", ARRIVE[c], [], None, sem=("big" + wn, ne * WAYS * len(rounds(c))), after=last[-1:])
+        turn[0] = (c + 1) * NBT - EARLY
         frames[wn] = frame(wn, small, small, [small, big], 400.0)
+        turn[0] = -NBT - 1
+    zp = fill(64, T.pw[:], 0.0, late=4000)
+    for e, o in ((0, 0), (1, 32), (2, 16)):
+        PW = gi(T.pw[64:128, 9 + e:105:12], [[-1, 8]], -o, 1, 1.0, [zp], [later])
 
-    def update(src, tt, pb, nb, deps):
-        mt = mm(64, deps + [EG], [(pb[:, 0:nb], eg[:], src, True, True)])
-        return ts(nb, [mt, khi], tt, pb[:, 0:nb], col(KLO), col(NK), A.max, A.min, late=-400)
-
-    def finish(dst_lo, dst_hi, tt, pa, nb, deps, last):
-        n4 = op("V", 60 + max(64, 2 * nb) * CY, deps, lambda: V.tensor_tensor(dst_hi, tt[0:64, :], tt[64:128, :], A.min), -400, drain=True)
+    def update(src, dst, a, pa, pb, nb, deps, last):
+        mt = mm(128, deps + EG + ZB, [(pb[:, 257 + t:256 + 3 * nb:3], eg[:, 128 * t:128 * t + 128], src, True, True) for t in range(2)])
+        new = v(3 * nb, [mt] + LIM, lambda: V.tensor_tensor_scan(dst[:, a:a + 3 * nb], pb[:, 256:256 + 3 * nb], T.lim[:, 0:3 * nb],
+                                                                 0.0, A.min, A.max))
         if last:
-            return n4
-        mf = mm(64, deps + FM, [(pa[0:64, 0:nb], T.fm[:], tt[:], True, True)])
-        return v(nb, [n4, mf], lambda: V.tensor_tensor(dst_lo, dst_hi, pa[0:64, 0:nb], A.mult), -400)
+            return mt, new
+        mf = mm(64, [new] + FM, [(pa[0:64, 0:nb], T.fm[:], dst[:, a + 2:a + 3 * nb:3], True, True)])
+        return mt, v(nb, [mf], lambda: V.tensor_tensor(dst[0:64, a + 2:a + 3 * nb:3], dst[64:128, a + 2:a + 3 * nb:3], pa[0:64, 0:nb], A.mult))
 
-    init = finish(T.i1[0:64, :], T.i1[64:128, :], T.ti, T.pa0, 64, [update(T.i0[:], T.ti[:], T.pb0, 64, [d0])], False)
+    init = update(T.i0[:], T.i1, 0, T.pa0, T.pb0, 64, [d0], False)[1]
 
     prev = [init] * NBT
-    bank = [init] * NBT
-    mbs = [T["mb0_%d" % i] for i in range(NBT)]
+    mbs = [T["mb%d" % i] for i in range(NBT)]
     fo, to = [], []
 
     def trail(i, hs, deps, after):
-        nb, w = BATCH[i], -(-BATCH[i] // 8) * 8
-        return mm(64 * len(hs), deps + [PW], [(T["pa%d" % i][0:96, 0:nb], T.pw[:, 9 - 3 * h:105 - 3 * h], mbs[i][:, h * w:h * w + nb],
-                                               h == 0, h == N - 1) for h in hs], after)
+        nb = BATCH[i]
+        return mm(64 * len(hs), deps + [PW], [(T["pa%d" % i][0:96, 0:nb], T.pw[:, 9 - 3 * h:105 - 3 * h],
+                                               mbs[i][:, 3 * h * nb + 2:3 * (h + 1) * nb:3], h == 0, h == N - 1) for h in hs], after)
 
     for h in range(N):
-        win, oh, wz, OH, WZ, pyr = frames[STEPS[h][0]]
+        win, oh, wz, OH, WZ, pyr = frames[STEPS[h]]
         for i, nb in enumerate(BATCH):
-            w = -(-nb // 8) * 8
             pa, pb, mb = T["pa%d" % i], T["pb%d" % i], mbs[i]
-            uv, off, gt, sc, tt = (T["%s%d_%d" % (x, h, i)] for x in ("uv", "off", "gt", "sc", "tt"))
-            sb, sa = (T.i1, B0[i]) if h == 0 else (mb, (h - 1) * w)
-            src = sb[:, sa:sa + nb]
-            oa = h * w
-            clr = [fill(1, mb[:, oa:oa + w], 0.0, late=1000)] if h == N - 1 or w != nb else []
-            m1 = mm(128, [prev[i], bank[i]] + L1, [(pb[:, 0:nb], T.l1[:, 0:128], src, True, True),
+            uv, off, gt, sc = (T["%s%d_%d" % (x, h, i)] for x in ("uv", "off", "gt", "sc"))
+            sb, sa = (T.i1, 3 * B0[i]) if h == 0 else (mb, 3 * (h - 1) * nb)
+            src = sb[:, sa + 2:sa + 3 * nb:3]
+            turn[0] = (h - 1) * NBT + i
+            m1 = mm(128, [prev[i]] + L1, [(pb[:, 0:nb], T.l1[:, 0:128], src, True, True),
                                                    (pb[:, nb:2 * nb], T.l1[:, 128:256], src, True, True)])
             rd = v(2 * nb, [m1], lambda uv=uv, pb=pb, nb=nb: V.tensor_copy(uv[:], pb[:, 0:2 * nb]), -300)
             cv = []
-            for hf, ps in enumerate((pa, pb)):
-                calls = []
-                for k in range(2):
-                    nh = 2 * hf + k
-                    o = ps[:, k * nb:(k + 1) * nb]
-                    calls.append((o, oh[:, 128 * nh:128 * nh + 128], uv[:, 0:nb], True, False))
-                    calls.append((o, oh[:, 512 + 128 * nh:640 + 128 * nh], uv[:, nb:2 * nb], False, True))
-                m2 = mm(256, [rd, OH[hf], OH[2 + hf]], calls)
-                cv.append(ts(2 * nb, [m2], off[:, 2 * hf * nb:2 * (hf + 1) * nb], ps[:, 0:2 * nb], -float(UM + MV[3]), None, A.add, late=-300))
-            ca = min(max(2 * int(round(ACT_SHARE[i] * 2 * nb)), 2 * nb), 4 * nb)
-
-            def need(a, b):
-                return [cv[x] for x in range(2) if a < 2 * (x + 1) * nb and b > 2 * x * nb] + pyr
-
+            for ps, qs in ((pa, (0, 1)), (pb, (2, 3))) if SPLIT else ((pa, (0, 1, 2, 3)),):
+                m2 = mm(128 * len(qs), [rd] + [OH[2 * c + x // 2] for c in range(2) for x in qs],
+                        [(ps[:, k * nb:(k + 1) * nb], oh[:, 512 * c + 128 * x:512 * c + 128 * x + 128], uv[:, c * nb:(c + 1) * nb], c == 0, c == 1)
+                         for k, x in enumerate(qs) for c in range(2)])
+                cv.append(ts(len(qs) * nb, [m2], off[:, qs[0] * nb:(qs[-1] + 1) * nb], ps[:, 0:len(qs) * nb], -float(UM + MV[3]), None, A.add))
+            turn[0] = h * NBT + i
+            cuts = [0, 2 * int(round(VSHARE[h] * 2 * nb))] + [x * nb for x in CUTS]
             ga = []
-            for a in range(ca, 4 * nb, GP):
-                b = min(a + GP, 4 * nb)
-                ga.append((a, b, op("V", 50, need(a, b), lambda a=a, b=b, gt=gt, off=off, win=win:
-                                    V.tensor_copy(gt[:, 16 * a:16 * b], win[:, 0:WIN].indirect(off[:, a:b])), ge=16 * (b - a))))
-            pieces = [(max(ca, 3 * nb), 4 * nb), (ca, 3 * nb)]
-            for nh in range(4):
-                a, b = nh * nb, min((nh + 1) * nb, ca)
-                if a < b:
-                    pieces.append((a, b))
-                    ga.append((a, b, op("A", 65, need(a, b), lambda a=a, b=b, gt=gt, off=off, win=win:
-                                        S.activation(gt[:, 16 * a:16 * b], win[:, 0:WIN].indirect(off[:, a:b]), AF.Copy), ge=16 * (b - a))))
-            scs = [(a, b, v(8 * (b - a), [k for x, y, k in ga if x < b and y > a] + [iseg], lambda a=a, b=b, gt=gt, sc=sc:
-                            V.tensor_tensor_scan(sc[:, 16 * a:16 * b], T.seg[:, 0:16 * (b - a)], gt[:, 16 * a:16 * b], 0.0, A.min, A.max), -100))
-                   for a, b in pieces if a < b]
+            for a, b in zip(cuts, cuts[1:]):
+                need = [cv[0]] * (a < 2 * nb) + [cv[-1]] * (b > 2 * nb) + pyr
+                cells, out = win[:, 0:WIN].indirect(off[:, a:b]), gt[:, 16 * a:16 * b]
+                if a:
+                    ga.append(op("A", 65, need, lambda out=out, cells=cells: S.activation(out, cells, AF.Copy), ge=16 * (b - a)))
+                else:
+                    ga.append(op("V", 50, need, lambda out=out, cells=cells: V.tensor_copy(out, cells), ge=16 * (b - a)))
+            cuts, ga = [0] + cuts[2:], [ga[0:2]] + [[x] for x in ga[2:]]
             pz = pa[0:24, 0:nb]
             z = mm(32, [cv[0], CZ], [(pz, T.cz[:, 0:24], src, True, False)])
-            for j, nh in enumerate([3, 0, 1, 2] if ca <= 3 * nb else [0, 1, 2, 3]):
-                calls = [(pz, wz[:, 4 * nh + n4:384:16], sc[:, 16 * nh * nb + 4 * n4 + 3:16 * (nh + 1) * nb:16], False,
-                          j == 3 and n4 == 3) for n4 in range(4)]
-                z = mm(4 * max(24, nb), [k for x, y, k in scs if x < (nh + 1) * nb and y > nh * nb] + WZ, calls, after=[z])
+            scs = []
+            for a, b, ks in zip(cuts, cuts[1:], ga):
+                scs.append(v(8 * (b - a), ks + [iseg], lambda a=16 * a, b=16 * b, gt=gt, sc=sc:
+                             V.tensor_tensor_scan(sc[:, a:b], T.seg[:, 0:b - a], gt[:, a:b], 0.0, A.min, A.max)))
+                z = mm(4 * (b - a) // nb * max(24, nb), scs[-1:] + WZ,
+                       [(pz, wz[:, :, n:128:16], sc[:, 16 * nb * (n // 4) + 4 * (n % 4) + 3:16 * nb * (n // 4 + 1):16], False, n == 15)
+                        for n in range(4 * a // nb, 4 * b // nb)], after=[z])
             if h == N - 1:
-                alls = [k for x, y, k in scs]
                 for n4 in range(4):
                     o, s = T.ft[:, n4:16:4, B0[i]:B0[i] + nb], sc[:, 4 * n4 + 3:64 * nb:16]
-                    fo.append(act(4 * nb, alls, o, s) if n4 % 2 else v(2 * nb, alls, lambda o=o, s=s: V.tensor_copy(o, s)))
-            n1 = ts(nb, [z, m1], sb[0:24, sa:sa + nb], pz, 92160.0, 104448.0, A.max, A.min, late=-400)
-            n3 = update(src, tt[:], pb, nb, [n1, cv[1]])
+                    fo.append(act(4 * nb, scs, o, s) if n4 % 2 else v(2 * nb, scs, lambda o=o, s=s: V.tensor_copy(o, s)))
+            n1 = ts(nb, [z, m1], sb[0:24, sa + 2:sa + 3 * nb:3], pz, 92160.0, 104448.0, A.max, A.min, late=-400)
+            mt, prev[i] = update(src, mb, 3 * h * nb, pa, pb, nb, [n1, cv[-1]], h == N - 1)
             if h == N - 1:
-                hist = trail(i, range(N - 1), [n1], [n3 - 1])
-            bank[i] = prev[i] = finish(mb[0:64, oa:oa + nb], mb[64:128, oa:oa + nb], tt, pa, nb, [n3] + clr, h == N - 1)
-            if h == N - 1:
+                hist = trail(i, range(N - 1), [n1], [mt])
                 to.append(act(nb, [trail(i, [h], [prev[i]], [hist])], T.tr[0:96, B0[i]:B0[i] + nb], pa[0:96, 0:nb]))
-            if STEPS[h][1]:
-                mbs[i] = T["mb%d_%d" % (h + 1, i)]
-                dst, sem = peer(STEPS[h][1]), "ar%d_%d" % (h + 1, i)
-                ne = len(topo.engines(core, dst))
-                nsent[0] += ne
-                s = op("G", 600, [bank[i]], lambda a=mbs[i][:, 0:oa + w], b=mb[:, 0:oa + w], dst=dst, sem=sem:
-                       g.remote_dma(a, b, T.sem[sem], T.sem.sent, topo.addr(dst)[1], topo.addr(dst)[0], topo.mask(core, dst)),
-                       sem=(), after=last[-1:] + [PW])
-                prev[i] = op("X", 0, [], None, sem=(sem, ne), after=[s], hp=1)
 
     op("Y", 3000, fo, lambda: Y.dma_start(T.feat[:], T.ft[:]), sem=("dft", 16))
     op("A", 2000, to, lambda: S.dma_start(T.trail[:], T.tr[0:96, :]), sem=("dtr", 16))

@@ -5,39 +5,53 @@ from concourse.mybir import AluOpType as A, ActivationFunctionType as AF
 N = 4
 SIM = 112
 BATCH = [22, 22, 20]
-VSHARE = [0.22] * 4
-SPLIT = False
+VSHARE = [0.24, 0.23, 0.24, 0.3]
+VPARTS = 1
+SPLIT = True
 CUTS = [2, 3, 4]
 SEG = 16 * max(BATCH) * max(b - a for a, b in zip([0] + CUTS, CUTS))
-PLANFOR = [(3000, 1.2, 50., 90.), (4000, 1.56, 70., 130.), (3500, 1.9, 60., 110.), (5000, 1.4, 120., 220.)]
-STARTS, TRIES = 200, 60000
-EARLY = 4.5
-LOADED = [3000, 4000, 5200, 6400]
-ARRIVE = [4500, 9500, 14500]
+PLANFOR = [(1500, 1.2, 70., 130.), (0, 1.5, 100., 180.), (3000, 1.8, 70., 130.), (2500, 1.35, 130., 250.)]
+STARTS, TRIES = 200, 130000
+EARLY, LONG, HEAT = 4.5, 2.0, 40.0
+AHEAD = 2
+LOADED = [2700, 3600, 3100, 2700]
+ARRIVE = [5000, 10000, 15000]
 STEPS = ["win", "win1", "win2", "win3"]
 COPIES = [(-h, STEPS[h]) for h in range(1, N)]
 NBT = len(BATCH)
 B0 = [sum(BATCH[:i]) for i in range(NBT)]
-MV = [8256, 7168, 2176, 1984]
+MV = [8256, 7168, 2080, 1984]
 LV = [(0, 4096), (4096, 1024), (5120, 256), (5376, 64)]
 WIN = MV[0] - MV[3] + 4096
 SMALL = MV[2] - MV[3] + 256
-WAYS, SUB = 7, 2
-CW = 372
-BIG = WIN - WAYS * SUB * CW
-CALLS = [(s, ws) for s in range(SUB) for ws in ((0, 1, 2, 3), (4, 5, 6))]
+PLAIN = [(far, False, i, i, False) for i in range(2) for far in (False, True)]
+PORT = [(True, True, i, i, False) for i in range(2)]
+LOW = (False, True, 0, 0, False)
+OWN = (False, True, 0, 0, True)
+CALLS = [(416, PLAIN), (352, PORT + [OWN]), (SMALL, [LOW] + PLAIN), (352, PORT + [OWN[:3] + (1, True)])]
+PART = 420
+PIECES = []
+_a = MV[1] - MV[3]
+for _j, (_w, _ps) in enumerate(CALLS):
+    for _p in _ps:
+        PIECES.append((_j, 0, _w) + _p if _p is LOW else (_j, _a, _a + _w) + _p)
+        _a += 0 if _p is LOW else _w
+HEADS = [LOW, PORT[0], PORT[1]]
+THIN = [2, 2, 2]
 UM = 160
-NK = 15
-KF, KF2, KM, KU0, KU1, KV0, KV1, KCZ, KUP, KL1, KL2, KX, KY, KS, KC = range(NK)
+NK = 14
+KF, KF2, KU0, KU1, KV0, KV1, KCZ, KUP, KL1, KL2, KX, KY, KS, KC = range(NK)
 KTAB = [(KF, 5, 1, 1, 0.5), (KF, 6, 1, 1, 0.25), (KF, 7, 2, 7 * NK, 0.125), (KF, 13, 1, 1, -38.0),
         (KF2, 5, 1, 1, 0.75), (KF2, 6, 1, 1, 0.1875), (KF2, 7, 1, 1, 3 / 64), (KF2, 13, 1, 1, -47.25), (KF2, 14, 1, 1, 1 / 64),
-        (KM, 5, 1, 1, 1088.0), (KM, 6, 1, 1, 4992.0), (KM, 7, 1, 1, 192.0), (KM, 13, 1, 1, -257024.0), (KM, 14, 1, 1, -320.0),
-        (KU0, 0, 1, 1, 1.0), (KU0, 14, 1, 1, float(UM)), (KU0, 15, 1, 1, -127 / 256), (KU1, 2, 1, 1, 1 / 16),
-        (KV0, 4, 1, 1, 64.0), (KV0, 1, 1, 1, -31.75), (KV0, 5, 1, 1, 1.0), (KV1, 3, 1, 1, 4.0),
+        (KU0, 8, 1, 1, 1.0), (KU0, 5, 1, 1, -160.0), (KU0, 6, 1, 1, -320.0), (KU0, 7, 1, 1, -640.0), (KU0, 2, 1, 1, 0.5),
+        (KU0, 3, 1, 1, 1.0), (KU0, 4, 1, 1, 2.0), (KU0, 9, 1, 1, 32640.0), (KU0, 13, 1, 1, -102.0), (KU0, 14, 1, 1, 1 / 32),
+        (KU1, 10, 1, 1, 1 / 16), (KV1, 10, 1, 1, 4.0),
+        (KV0, 12, 1, 1, 64.0), (KV0, 5, 1, 1, -20352.0), (KV0, 6, 1, 1, -4544.0), (KV0, 7, 1, 1, -93696.0), (KV0, 2, 1, 1, -32.0),
+        (KV0, 4, 1, 1, 128.0), (KV0, 9, 1, 1, 2867200.0), (KV0, 13, 1, 1, -1664.0), (KV0, 14, 1, 1, 2.0),
         (KCZ, 13, 1, 1, 12288.0), (KCZ, 14, 1, 1, -32.0), (KCZ, 15, 1, 1, 1 / 16),
-        (KUP, 5, 1, 1, 53.0), (KUP, 6, 1, 1, 41.0), (KUP, 7, 1, 1, 17.0), (KUP, 8, 2, 4 * NK, 60.0), (KUP, 10, 2, NK, 56.0),
+        (KUP, 2, 2, 3 * NK, 53.0), (KUP, 3, 2, 3 * NK, 41.0), (KUP, 4, 2, 3 * NK, 17.0), (KUP, 8, 2, 4 * NK, 60.0), (KUP, 10, 1, 1, 56.0),
         (KL1, 5, 2, 1, 52.0), (KL1, 6, 2, 1, 40.0), (KL1, 7, 2, 1, 16.0), (KL1, 8, 2, 4 * NK, 8.0),
-        (KL1, 10, 2, 1, 4.0), (KL1, 11, 2, 1, 4.0),
+        (KL1, 2, 2, 1, 52.0), (KL1, 3, 2, 1, 40.0), (KL1, 4, 2, 1, 16.0), (KL1, 10, 2, 1, 4.0),
         (KUP, 9, 3, 1, 1.0), (KUP, 13, 3, 1, 1.0), (KUP, 14, 3, 1, 1.0), (KUP, 15, 3, 1, 1.0),
         (KX, 0, 3, NK + 1, 1 / 512), (KX, 14, 3, 1, -192.0), (KX, 8, 2, 2 * NK + 2, 1.0), (KY, 12, 1, 1, 1.0),
         (KC, 2, 1, 1, -1 / 512), (KC, 10, 1, 1, -1.0), (KC, 14, 1, 1, 256.0)]
@@ -47,12 +61,12 @@ BF = "bfloat16"
 SCRATCH = {"sxy": ("sbuf", [128, 16], "int32"), "bx": ("sbuf", [128, 64], "int32"), "pi": ("sbuf", [128, 4], "int32"),
            "kc": ("sbuf", [128, 16], "float32"), "pf": ("sbuf", [128, 4], "float32"), "mg": ("sbuf", [128, 8], "float32"),
            "tr": ("sbuf", [128, 64], "float32"), "ft": ("sbuf", [128, 16, 64], BF)}
-for _k, _n in dict(krow=16 * NK, zrow=256, icol=128, jrow=128, grow=128, g8=80, mkl=128, tmpl=256, l1=256, fm=64, cz=32,
+for _k, _n in dict(krow=16 * NK, zrow=256, icol=128, jrow=128, grow=128, g8=80, mkl=128, tmpl=256, l1=256, fm=256, cz=32,
                    eg=256, pw=112, seg=SEG, i0=64, i1=192, lim=192).items():
     SCRATCH[_k] = ("sbuf", [128, _n], BF)
 for _w in ["win"] + [_c[1] for _c in COPIES]:
     SCRATCH["wz" + _w] = ("sbuf", [128, 3, 128], BF)
-    for _k, _n in (("", WIN), ("ot", 1024), ("oh", 1024)):
+    for _k, _n in (("", WIN), ("hd", 64), ("ot", 1024), ("oh", 1024)):
         SCRATCH[_k + _w] = ("sbuf", [128, _n], BF)
 for _i, _nb in enumerate(BATCH):
     SCRATCH["pa%d" % _i] = ("psum", [128, 512], "float32")
@@ -60,11 +74,12 @@ for _i, _nb in enumerate(BATCH):
     SCRATCH["mb%d" % _i] = ("sbuf", [128, N * 3 * _nb], BF)
     for _h in range(N):
         SCRATCH["off%d_%d" % (_h, _i)] = ("sbuf", [128, 4 * _nb], "uint16")
-        for _k, _n in (("uv", 2), ("gt", 64), ("sc", 64)):
+        for _k, _n in (("uv", 2), ("ff", 2), ("gt", 64), ("sc", 64)):
             SCRATCH["%s%d_%d" % (_k, _h, _i)] = ("sbuf", [128, _n * _nb], BF)
-SEMAPHORES = (["cP", "cV", "cA", "cG", "dp0", "dhd", "dsxy", "dbx", "dft", "dtr", "sent"] + ["dw" + w for w in STEPS[1:]]
-              + [x + c[1] for c in COPIES for x in ("small", "big")] + ["ch%d" % s for s in range(SUB)]
-              + ["dp%d" % (j + 1) for j in range(len(CALLS))] + ["rl%d_%d" % (c, s) for c in range(N - 1) for s in range(SUB)])
+SEMAPHORES = (["cP", "cV", "cA", "cG", "dhd", "dsxy", "dbx", "dft", "dtr", "sent", "head"]
+              + [x + c[1] for c in COPIES for x in ("small", "big")] + ["ch%d" % j for j in range(len(CALLS) + 1)]
+              + ["dp%d" % (j + 1) for j in range(len(CALLS))] + ["dw" + w for w in STEPS[1:]]
+              + ["rl%d_%d_%d" % (c, k, p) for c in range(N - 1) for k, x in enumerate(PIECES) for p in range(-(-(x[2] - x[1]) // PART))])
 CY = 1.04
 
 
@@ -75,7 +90,7 @@ def plan(ops):
     cases = [([[(d, l1 if q[d] == q[k] else l2) for d in o["deps"]] + [(d, 0.) for d in o["after"]] for k, o in enumerate(ops)],
               [o["cost"] + o["ge"] * gc * CY + o["hp"] * hop for o in ops]) for hop, gc, l1, l2 in PLANFOR]
     tail = [o["tail"] for o in ops]
-    urge = [k for k, o in enumerate(ops) if o["sem"] == ()][:1 + len(CALLS)]
+    urge = [k for k, o in enumerate(ops) if o["sem"] == ()][:len(CALLS) + 1]
 
     def replay(order, case):
         dep, cost = case
@@ -105,7 +120,7 @@ def plan(ops):
     for k in range(n):
         for d in pre[k]:
             suc[d].append(k)
-    first = None
+    first = []
     for it in range(STARTS):
         dep, cost = cases[it % len(cases)]
         rest = [0.] * n
@@ -113,8 +128,8 @@ def plan(ops):
             rest[k] += cost[k]
             for d, l in dep[k]:
                 rest[d] = max(rest[d], rest[k] + l)
-        win, noise = (0, 50, 100, 200)[int(rnd() * 4)], (0, 100, 300)[int(rnd() * 3)]
-        pri = [1e9 - k if tail[k] else 0.2 * rest[k] + noise * rnd() - 1e5 * ops[k]["turn"] for k in range(n)]
+        win, noise, step = 300 * rnd(), 300 * rnd(), (1e5, 1e3, 500.)[int(rnd() * 3)]
+        pri = [1e9 - k if tail[k] or k in urge else 0.2 * rest[k] + noise * rnd() - step * ops[k]["turn"] - LONG * cost[k] for k in range(n)]
         left = [len(p) for p in pre]
         ready = {k: 0. for k in range(n) if not left[k]}
         end, free, o = [0.] * n, [0.] * 6, []
@@ -131,19 +146,51 @@ def plan(ops):
                 left[s] -= 1
                 if not left[s]:
                     ready[s] = max(end[d] + l for d, l in dep[s])
-        val = value(o)[0]
-        if first is None or val < first[0]:
-            first = (val, o)
-    order = first[1]
-    cur, runs = value(order)
-    low, kept = cur, order
+        first.append((value(o)[0], o))
+    first.sort()
+    low, kept = first[0]
+
+    def critical(runs):
+        out = []
+        for end, why, res in runs:
+            k = end.index(max(end))
+            while k >= 0:
+                if res[k] and why[k] >= 0 and why[k] not in pre[k]:
+                    out.append(k)
+                k = why[k]
+        return out
+
+    def again(o, pa, bound):
+        seen, tot, new, rest = {q[k]: k for k in o[:pa]}, 0., [], o[pa:]
+        for i, (dep, cost) in enumerate(cases):
+            end, free = ends[i][:], [0.] * 6
+            for e, k in seen.items():
+                free[e] = (end[k] - tail[k]) * (e != 5)
+            new.append(end)
+            for k in rest:
+                e = q[k]
+                t = free[e]
+                for d, l in dep[k]:
+                    if end[d] + l > t:
+                        t = end[d] + l
+                end[k] = t = t + cost[k]
+                if e != 5:
+                    free[e] = t - tail[k]
+            tot += max(end) + sum(0.2 * end[k] for k in urge) - olds[i]
+            if tot > bound + 150. * (len(cases) - 1 - i):
+                return None
+        return new
+
+    def each(ends):
+        return [max(x) + sum(0.2 * x[k] for k in urge) for x in ends]
+
+    order = kept
+    ends = [x[0] for x in value(order)[1]]
+    olds = each(ends)
     for it in range(TRIES):
-        end, why, res = runs[int(rnd() * len(runs))]
-        k, crit = end.index(max(end)), []
-        while k >= 0:
-            if res[k] and why[k] >= 0 and why[k] not in pre[k]:
-                crit.append(k)
-            k = why[k]
+        heat = HEAT * (1 - it / TRIES)
+        if it % 16 == 0:
+            crit = critical([replay(order, cases[it // 16 % len(cases)])])
         b = crit[int(rnd() * len(crit))] if crit and rnd() > 0.25 else order[int(rnd() * n)]
         pb = order.index(b)
         same = [x for x in order[max(0, pb - 40):pb] if q[x] == q[b]]
@@ -169,65 +216,54 @@ def plan(ops):
         if a in grp and b in grp:
             continue
         o2 = order[:pa] + new + order[pb + 1:]
-        val, r2 = value(o2)
-        if val < cur or rnd() < math.exp((cur - val) / (100.0 * (1 - it / TRIES) + 5)):
-            order, cur, runs = o2, val, r2
+        got = again(o2, pa, -len(cases) * (heat + 3) * math.log(rnd() + 1e-9))
+        if got:
+            order, ends, olds = o2, got, each(got)
+            cur = sum(olds) / len(olds)
             if cur < low:
                 low, kept = cur, order
     return kept, [max(replay(kept, c)[0]) for c in cases], replay(kept, cases[1])[0]
 
 
-def holders(src, T, topo):
+def holder(src, k, c, T, topo):
+    return src if PIECES[k][7] and not c else held_by(src, PIECES[k][3:], T, topo)
+
+
+def held_by(src, entry, T, topo):
+    far, port, idx = entry[:3]
     other = T.cores[(T.rank_of(src) + 1) % N]
-    own = [x for x in topo.cores_of(src) if x != src]
-
-    def pick(near, port):
-        return [x for x in own if (topo.die(x) == topo.die(src)) == near and topo.may_write(x, other) == port]
-    a, b = pick(True, False), pick(False, False)
-    return pick(True, True)[0], [a[0], b[0], a[1], b[1]] + pick(False, True) + [src]
+    return [x for x in topo.cores_of(src) if x != src and (topo.die(x) != topo.die(src)) == far and topo.may_write(x, other) == port][idx]
 
 
-def relay(w, src, dst, T, topo):
-    x = holders(src, T, topo)[1][w]
-    port = topo.may_write(x, T.cores[(T.rank_of(src) + 1) % N])
+def relay(src, dst, k, T, topo):
+    j, a, b, far, port, idx, hand, spare = PIECES[k]
     if port != topo.same_plane(topo.chip(src), topo.chip(dst)):
         return None
-    on = [y for y in range(SIM) if topo.mates(topo.chip(y), topo.chip(dst)) and topo.die(y) == topo.die(x) and topo.may_write(y, dst)]
-    return on[(0, 0, 1, 1, 0, 1, 0)[w]]
+    return [y for y in range(SIM) if topo.mates(topo.chip(y), topo.chip(dst)) and (topo.die(y) != topo.die(src)) == far
+            and topo.may_write(y, dst)][hand]
 
 
-def piece(t, s, w):
-    a = BIG + (s * WAYS + w) * CW
-    return t[:, a:a + CW]
+def call_engines(src, j, T, topo):
+    ks = [k for k, p in enumerate(PIECES) if (p[0] == j if j < len(CALLS) else p[7])]
+    every, off = topo.engines(src, holder(src, 0, 0, T, topo)), topo.engines(src, T.cores[(T.rank_of(src) + 1) % N])
+    own = [k for k in ks if PIECES[k][7] and j < len(CALLS)]
+    near, far = ([k for k in ks if k not in own and PIECES[k][3] == x] for x in (False, True))
+    rest = [e for e in every if e not in off or not own]
+    sets = [(own, off)] * bool(own) + ([(near, rest[1::2]), (far, rest[0::2])] if near and far else [(near + far, rest)])
+    out = {}
+    for x, eng in sets:
+        share = 1 << (len(x) - 1).bit_length()
+        for i, k in enumerate(x):
+            out[k] = eng[i * len(eng) // share:(i + 1) * len(eng) // share if i + 1 < len(x) else None]
+    return out
 
 
-def rounds(c):
-    return [[s] for s in range(SUB)]
+def thin(c, k):
+    return 1 if c == 0 and PIECES[k][4] else 2
 
 
-def transfer(T, topo, to, eng, sem, src, dst):
-    rid, pid, _ = topo.addr(to)
-    return RemoteDMATransfer(dst_ids=[DstId(rid=rid, pnc=pid)], dma_engine_mask=sum(1 << e for e in eng), remote_sem=T.sem[sem],
-                             src=src, dst=dst)
-
-
-def onward(T, topo, core, src, c, w, j, via):
-    d, wn = COPIES[c]
-    dst = T.cores[(T.rank_of(src) + d) % N]
-    r = relay(w, src, dst, T, topo) if via else None
-    to, sem = (dst, "big" + wn) if r is None else (r, "rl%d_%d" % (c, j))
-    eng, ss = topo.engines(core, to), rounds(c)[j]
-    return [transfer(T, topo, to, eng[i::len(ss)], sem, piece(T.win if via else T[wn], s, w), piece(T[wn], s, w)) for i, s in enumerate(ss)]
-
-
-def call_engines(src, T, topo, ws):
-    first, hold = holders(src, T, topo)
-    every, off = topo.engines(src, first), topo.engines(src, T.cores[(T.rank_of(src) + 1) % N])
-    if src not in [hold[w] for w in ws]:
-        half = len(every) // 2
-        return [every[half * (p // 2):half * (p // 2 + 1)][1 - p % 2::2] for p in range(len(ws))]
-    rest = [e for e in every if e not in off]
-    return [off if hold[w] == src else rest[p::2] for p, w in enumerate(ws)]
+def parts(k, via):
+    return 1 if via is None else -(-(PIECES[k][2] - PIECES[k][1]) // PART)
 
 
 def helper(g, core, T, topo):
@@ -235,33 +271,33 @@ def helper(g, core, T, topo):
     for c, (d, wn) in enumerate(COPIES):
         for r in range(N):
             src, dst = T.cores[r], T.cores[(r + d) % N]
-            first, hold = holders(src, T, topo)
-            ne = len(topo.engines(src, dst))
-            if core == first:
-                if c == 0:
-                    g.wait_ge(T.sem.ch0, len(topo.engines(src, core)))
-                g.remote_dma_fused([transfer(T, topo, dst, topo.engines(core, dst), "small" + wn, T.win[:, 0:SMALL], T[wn][:, 0:SMALL])],
-                                   local_sem=T.sem.sent)
-                n += ne
+            if core == held_by(src, HEADS[c], T, topo):
+                g.wait_ge(T.sem.head, len(topo.engines(src, core)[c::4]))
+                g.remote_dma(T["hd" + wn][:], T.hdwin[:], T.sem["small" + wn], T.sem.sent, topo.addr(dst)[1], topo.addr(dst)[0], topo.mask(core, dst))
+                n += len(topo.engines(core, dst))
     for c, (d, wn) in enumerate(COPIES):
         for r in range(N):
             src, dst = T.cores[r], T.cores[(r + d) % N]
-            first, hold = holders(src, T, topo)
-            for w in range(WAYS):
-                via = core == (first if c and hold[w] == src else hold[w])
-                if not via and core != relay(w, src, dst, T, topo):
+            for k in range(len(PIECES)):
+                j, a, b, far = PIECES[k][:4]
+                via = relay(src, dst, k, T, topo)
+                held = core == holder(src, k, c, T, topo)
+                if not held and core != via:
                     continue
-                for j in range(len(rounds(c))):
-                    if not via:
-                        g.wait_ge(T.sem["rl%d_%d" % (c, j)], ne)
-                    elif core == first:
-                        if c == 1 and j == 0:
-                            g.wait_ge(T.sem.ch1, len(topo.engines(src, core)))
-                    elif c == 0:
-                        ws = [x for s, x in CALLS if w in x][0]
-                        g.wait_ge(T.sem["ch%d" % j], len(call_engines(src, T, topo, ws)[ws.index(w)]))
-                    g.remote_dma_fused(onward(T, topo, core, src, c, w, j, via), local_sem=T.sem.sent)
-                    n += ne
+                to = via if held and via is not None else dst
+                eng = topo.engines(core, to)[::thin(c, k)]
+                if held and c == 0:
+                    g.wait_ge(T.sem["ch%d" % j], sum(len(e) for x, e in call_engines(src, j, T, topo).items() if holder(src, x, 0, T, topo) == core))
+                if held and c == 1 and PIECES[k][7]:
+                    g.wait_ge(T.sem["ch%d" % len(CALLS)], sum(len(e) for e in call_engines(src, len(CALLS), T, topo).values()))
+                m = parts(k, via)
+                for p in range(m):
+                    lo, hi, stop = a + (b - a) * p // m, a + (b - a) * (p + 1) // m, "rl%d_%d_%d" % (c, k, p)
+                    if not held:
+                        g.wait_ge(T.sem[stop], len(eng))
+                    g.remote_dma(T[wn][:, lo:hi], T["win" if held else wn][:, lo:hi], T.sem[stop if to != dst else "big" + wn],
+                                 T.sem.sent, topo.addr(to)[1], topo.addr(to)[0], sum(1 << e for e in eng))
+                    n += len(eng)
     if n:
         g.wait_ge(T.sem.sent, n)
 
@@ -300,8 +336,8 @@ def build(g, T, topo, core):
             return r
         return op("P", n * CY, deps, fn, after=after)
 
-    def load(q, out, in_, sem, cost):
-        return op(q, cost, [], lambda: (S if q == "A" else Y).dma_start(out, in_), -1e4, sem=sem, tail=cost - 100)
+    def load(q, out, in_, sem, cost, deps=()):
+        return op(q, cost, deps, lambda: (S if q == "A" else Y).dma_start(out, in_), -1e4, sem=sem, tail=cost - 100)
 
     kc = T.kc
 
@@ -310,20 +346,20 @@ def build(g, T, topo, core):
 
     load("A", T.sxy[:, 0:4], T.sx[:], ("dsxy", 16), 2000)
     dsy = load("A", T.sxy[:, 4:8], T.sy[:], ("dsxy", 32), 2000)
-    dhd = load("A", T.win[:, 64:112], T.head[:], ("dhd", 16), 2000)
+    dhd = load("A", T.hdwin[:, 0:48], T.head[:], ("dhd", 16), 2000)
     for e in range(3):
         dbx = load("A", T.bx[8 * e:8 * e + 8, :], T.box[:, 64 * e:64 * e + 64], ("dbx", 16 * (e + 1)), 2000)
-    for j, l in enumerate((3, 2)):
-        dp0 = load("Y", T.win[:, MV[l] - MV[3]:MV[l] - MV[3] + LV[l][1]], T.pyr[:, LV[l][0]:LV[l][0] + LV[l][1]], ("dp0", 16 * (j + 1)), 2200)
     dps = []
-    for j, (s, ws) in enumerate(CALLS):
-        lo, hi, n = BIG + (s * WAYS + ws[0]) * CW, BIG + (s * WAYS + ws[-1] + 1) * CW, 0
-        for l in (1, 0):
-            a, b = max(lo, MV[l] - MV[3]), min(hi, MV[l] - MV[3] + LV[l][1])
+    for j in range(len(CALLS)):
+        mine, n = [p for p in PIECES if p[0] == j], 0
+        lo, hi = min(p[1] for p in mine if p[1]), max(p[2] for p in mine)
+        for l in range(4):
+            a, b = MV[l] - MV[3], MV[l] - MV[3] + LV[l][1]
+            a, b = (max(lo, a), min(hi, b)) if l < 2 else (a, b * (LOW in CALLS[j][1]))
             if a < b:
                 n += 1
                 o = LV[l][0] - MV[l] + MV[3]
-                dp = load("Y", T.win[:, a:b], T.pyr[:, a + o:b + o], ("dp%d" % (j + 1), 16 * n), LOADED[j])
+                dp = load("Y", T.win[:, a:b], T.pyr[:, a + o:b + o], ("dp%d" % (j + 1), 16 * n), LOADED[j], dps[-AHEAD:1 - AHEAD])
         dps.append(dp)
 
     zk = fill(8 * NK, T.krow[0:1, :], 0.0, late=-600)
@@ -368,9 +404,7 @@ def build(g, T, topo, core):
     LIM = [ts(1, [kcp, iic], T.lim[:, t:192:3], T.icol[:, 0:64], 0.0, col(KUP + t), A.mult, A.add) for t in range(3)]
     ZB = [fill(64, T["pb%d" % i][:, 256:448:3], 0.0) for i in range(NBT)]
     d0 = ts(64, [dbx, oi], T.i0[0:24, :], T.bx[0:24, :], 191.0, 512.0, A.add, A.mult, late=-500)
-    FM = [ts(1, [kcp, p3, ig8], T.fm[:, a:b], T.g8[:, 0:b - a], pm8, col(k), A.is_equal, A.mult)
-          for a, b, k in ((0, 24, KF), (24, 40, KF2), (40, 48, KM))]
-    FM.append(fill(1, T.fm[:, 48:64], 0.0))
+    FM = [ts(64, [kcp, p3, igr], T.fm[:, 128 * j:128 * j + 128], T.grow[:], pm8, col(k), A.is_equal, A.mult) for j, k in enumerate((KF, KF2))]
     EG = [ts(1, [kcp, p3, ig8], eg[:, 128 * t + a:128 * t + b], T.g8[:, 0:b - a], pm8, col(k), A.is_equal, A.mult, late=-500)
           for t in range(2) for a, b, k in NEWS[t]]
     ml = ts(64, [p3, igr], T.mkl[:], T.grow[:], pm8, None, A.is_equal)
@@ -379,71 +413,74 @@ def build(g, T, topo, core):
         tm = T.tmpl[:, 128 * j:128 * j + 128]
         t1 = ts(64, [kcp, ijr], tm, T.jrow[:], col(k1), col(k0), A.mult, A.add)
         L1.append(v(256, [t1, ml], lambda j=j, tm=tm: V.tensor_tensor(T.l1[:, 128 * j:128 * j + 128], tm, T.mkl[:], A.mult)))
-    sco = ts(8, [dsy, p3], T.win[:, 112:120], T.sxy[:, 0:8], p16, None, A.add)
+    sco = ts(8, [dsy, p3], T.hdwin[:, 48:56], T.sxy[:, 0:8], p16, None, A.add)
     CZ = ts(24, [kcp, iic], T.cz[:, 0:24], T.icol[:, 0:24], 0.0, col(KCZ), A.mult, A.add)
     mgk = ts(8, [p3, iic], T.mg[:], T.icol[:, 0:128:16], p16, None, A.is_equal)
 
     def frame(wn, d1, d2, pyr, late):
-        win, ot, oh, wz = T[wn], T["ot" + wn], T["oh" + wn], T["wz" + wn]
-        ots = [ts(64, [d1, iic], ot[:, 128 * j:128 * j + 128], T.icol[:], win[:, 112 + j:113 + j], None, A.is_equal, late=late)
+        win, hd, ot, oh, wz = T[wn], T["hd" + wn], T["ot" + wn], T["oh" + wn], T["wz" + wn]
+        ots = [ts(64, [d1, iic], ot[:, 128 * j:128 * j + 128], T.icol[:], hd[:, 48 + j:49 + j], None, A.is_equal, late=late)
                for j in range(8)]
         o = [v(128, ots[2 * j:2 * j + 2], lambda j=j: V.transpose(oh[:, 256 * j:256 * j + 256], ot[:, 256 * j:256 * j + 256]), late)
              for j in range(4)]
         if wn == STEPS[0]:
-            return win, oh, wz, o, [act(48, [mgk, d2], wz[:, :, 16 * j:16 * j + 16], win[:, 64:112], T.mg[:, j:j + 1]) for j in range(8)], pyr
+            return win, oh, wz, o, [act(48, [mgk, d2], wz[:, :, 16 * j:16 * j + 16], hd[:, 0:48], T.mg[:, j:j + 1]) for j in range(8)], pyr
         zero = act(384, [iseg], wz[:], T.seg[:, 0:384], 0.0)
+        ops[zero]["turn"] = -NBT - 0.5
         for j in range(8):
-            w = op("Y", 2000, [zero, d2], lambda j=j: Y.dma_start(wz[16 * j:16 * j + 16, :, 16 * j:16 * j + 16], win[16 * j:16 * j + 16, 64:112]),
+            w = op("Y", 2000, [zero, d2], lambda j=j: Y.dma_start(wz[16 * j:16 * j + 16, :, 16 * j:16 * j + 16], hd[16 * j:16 * j + 16, 0:48]),
                    sem=("dw" + wn, 16 * (j + 1)), tail=1900)
         return win, oh, wz, o, [w], pyr
 
     gaps = [fill((b - a) / 2, T.win[:, a:b], 0.0, late=-300)
-            for a, b in ((120, 192), (BIG, MV[1] - MV[3]), (MV[1] - MV[3] + LV[1][1], MV[0] - MV[3]))]
-    frames = {"win": frame("win", sco, dhd, [dp0, dhd, sco] + gaps + dps, 0.0)}
-    nsent = [0]
+            for a, b in ((LV[3][1], MV[2] - MV[3]), (MV[1] - MV[3] + LV[1][1], MV[0] - MV[3]))]
+    zh = fill(1, T.hdwin[:, 56:64], 0.0)
+    frames = {"win": frame("win", sco, dhd, gaps + dps, 0.0)}
 
-    first, hold = holders(core, T, topo)
+    def send(j):
+        trs = []
+        for k, eng in call_engines(core, j, T, topo).items():
+            to, wn, sem = holder(core, k, j == len(CALLS), T, topo), "win", "ch%d" % j
+            if to == core:
+                to, wn, sem = peer(COPIES[0][0]), COPIES[0][1], "big" + COPIES[0][1]
+            rid, pid, _ = topo.addr(to)
+            a, b = PIECES[k][1:3]
+            trs.append(RemoteDMATransfer(dst_ids=[DstId(rid=rid, pnc=pid)], dma_engine_mask=sum(1 << e for e in eng),
+                                         remote_sem=T.sem[sem], src=T.win[:, a:b], dst=T[wn][:, a:b]))
+        return g.remote_dma_fused(trs, local_sem=T.sem.sent)
 
-    def send(trs, n, deps, after):
-        nsent[0] += n
-        return op("G", 700, deps, lambda: g.remote_dma_fused(trs(), local_sem=T.sem.sent), -1e4, sem=(), after=after)
+    def heads():
+        to = [held_by(core, x, T, topo) for x in HEADS]
+        return g.remote_dma_fused([RemoteDMATransfer(dst_ids=[DstId(rid=topo.addr(x)[0], pnc=topo.addr(x)[1])], remote_sem=T.sem.head,
+                                                     dma_engine_mask=sum(1 << e for e in topo.engines(core, x)[c::4]), src=T.hdwin[:], dst=T.hdwin[:])
+                                   for c, x in enumerate(to)], local_sem=T.sem.sent)
 
-    every, ne = topo.engines(core, first), len(topo.engines(core, peer(1)))
-    last = [send(lambda: [transfer(T, topo, first, every, "ch0", T.win[:, 0:SMALL], T.win[:, 0:SMALL])], len(every),
-                 [dp0, dhd, sco, gaps[0]], [igr])]
-    for j, (s, ws) in enumerate(CALLS):
-        def trs(s=s, ws=ws):
-            out = []
-            for w, es in zip(ws, call_engines(core, T, topo, ws)):
-                if hold[w] == core:
-                    out += onward(T, topo, core, core, 0, w, s, True)
-                else:
-                    out.append(transfer(T, topo, hold[w], es, "ch%d" % s, piece(T.win, s, w), piece(T.win, s, w)))
-            return out
-        last.append(send(trs, len(every), [dps[j]] + gaps[1:], last[-1:]))
-    own = hold.index(core)
-    later = send(lambda: [transfer(T, topo, first, every[s::SUB], "ch1", piece(T.win, s, own), piece(T.win, s, own)) for s in range(SUB)],
-                 len(every), [], last[-1:])
+    last = [op("G", 700, [dhd, sco, zh], heads, sem=(), after=[igr])]
+    nsent = sum(len(topo.engines(core, held_by(core, x, T, topo))[c::4]) for c, x in enumerate(HEADS))
+    for j in range(len(CALLS) + 1):
+        last.append(op("G", 700, dps[j:j + 1] + gaps, lambda j=j: send(j), sem=(), after=last[-1:]))
+        nsent += sum(len(e) for e in call_engines(core, j, T, topo).values())
+    later = last[-1]
     for c, (d, wn) in enumerate(COPIES):
-        small = op("X", 6500 + 5000 * c, [], None, sem=("small" + wn, ne), after=last[:1])
-        big = op("X", ARRIVE[c], [], None, sem=("big" + wn, ne * WAYS * len(rounds(c))), after=last[-1:])
+        ne = len(topo.engines(peer(-d), core))
+        small, place = (op("X", t, [], None, sem=("small" + wn, ne), after=last[:1]) for t in (6500, 7500 + 4000 * c))
+        big = op("X", ARRIVE[c], [], None, sem=("big" + wn, sum(len(call_engines(core, p[0], T, topo)[k]) if p[7] and not c else
+                                                                 ne // thin(c, k) * parts(k, relay(peer(-d), core, k, T, topo))
+                                                                 for k, p in enumerate(PIECES))), after=[last[len(CALLS)]], hp=1)
         turn[0] = (c + 1) * NBT - EARLY
-        frames[wn] = frame(wn, small, small, [small, big], 400.0)
+        frames[wn] = frame(wn, small, place, [big], 400.0)
         turn[0] = -NBT - 1
     zp = fill(64, T.pw[:], 0.0, late=4000)
     for e, o in ((0, 0), (1, 32), (2, 16)):
         PW = gi(T.pw[64:128, 9 + e:105:12], [[-1, 8]], -o, 1, 1.0, [zp], [later])
 
-    def update(src, dst, a, pa, pb, nb, deps, last):
+    def update(src, dst, a, pb, nb, deps):
         mt = mm(128, deps + EG + ZB, [(pb[:, 257 + t:256 + 3 * nb:3], eg[:, 128 * t:128 * t + 128], src, True, True) for t in range(2)])
         new = v(3 * nb, [mt] + LIM, lambda: V.tensor_tensor_scan(dst[:, a:a + 3 * nb], pb[:, 256:256 + 3 * nb], T.lim[:, 0:3 * nb],
                                                                  0.0, A.min, A.max))
-        if last:
-            return mt, new
-        mf = mm(64, [new] + FM, [(pa[0:64, 0:nb], T.fm[:], dst[:, a + 2:a + 3 * nb:3], True, True)])
-        return mt, v(nb, [mf], lambda: V.tensor_tensor(dst[0:64, a + 2:a + 3 * nb:3], dst[64:128, a + 2:a + 3 * nb:3], pa[0:64, 0:nb], A.mult))
+        return mt, new
 
-    init = update(T.i0[:], T.i1, 0, T.pa0, T.pb0, 64, [d0], False)[1]
+    init = update(T.i0[:], T.i1, 0, T.pb0, 64, [d0])[1]
 
     prev = [init] * NBT
     mbs = [T["mb%d" % i] for i in range(NBT)]
@@ -462,26 +499,30 @@ def build(g, T, topo, core):
             sb, sa = (T.i1, 3 * B0[i]) if h == 0 else (mb, 3 * (h - 1) * nb)
             src = sb[:, sa + 2:sa + 3 * nb:3]
             turn[0] = (h - 1) * NBT + i
-            m1 = mm(128, [prev[i]] + L1, [(pb[:, 0:nb], T.l1[:, 0:128], src, True, True),
-                                                   (pb[:, nb:2 * nb], T.l1[:, 128:256], src, True, True)])
-            rd = v(2 * nb, [m1], lambda uv=uv, pb=pb, nb=nb: V.tensor_copy(uv[:], pb[:, 0:2 * nb]), -300)
+            ff = T["ff%d_%d" % (h, i)]
+            mf, m1 = (mm(128, [prev[i]] + w, [(ps[:, c * nb:(c + 1) * nb], t[:, 128 * c:128 * c + 128], src, True, True) for c in range(2)])
+                      for ps, t, w in ((pa, T.fm, FM), (pb, T.l1, L1)))
+            fs = v(2 * nb, [mf], lambda ff=ff, pa=pa, nb=nb: V.tensor_copy(ff[:], pa[:, 0:2 * nb]))
+            rd = v(2 * nb, [m1, fs], lambda uv=uv, pb=pb, ff=ff, nb=nb: V.tensor_tensor(uv[:], pb[:, 0:2 * nb], ff[:], A.mult))
             cv = []
             for ps, qs in ((pa, (0, 1)), (pb, (2, 3))) if SPLIT else ((pa, (0, 1, 2, 3)),):
-                m2 = mm(128 * len(qs), [rd] + [OH[2 * c + x // 2] for c in range(2) for x in qs],
-                        [(ps[:, k * nb:(k + 1) * nb], oh[:, 512 * c + 128 * x:512 * c + 128 * x + 128], uv[:, c * nb:(c + 1) * nb], c == 0, c == 1)
-                         for k, x in enumerate(qs) for c in range(2)])
-                cv.append(ts(len(qs) * nb, [m2], off[:, qs[0] * nb:(qs[-1] + 1) * nb], ps[:, 0:len(qs) * nb], -float(UM + MV[3]), None, A.add))
+                m2 = []
+                for k, x in enumerate(qs):
+                    m2 = [mm(128, [rd, OH[x // 2], OH[2 + x // 2]],
+                             [(ps[:, k * nb:(k + 1) * nb], oh[:, 512 * c + 128 * x:512 * c + 128 * x + 128], uv[:, c * nb:(c + 1) * nb], c == 0, c == 1)
+                              for c in range(2)], m2)]
+                cv.append(ts(len(qs) * nb, m2, off[:, qs[0] * nb:(qs[-1] + 1) * nb], ps[:, 0:len(qs) * nb], -float(UM + MV[3]), None, A.add))
             turn[0] = h * NBT + i
-            cuts = [0, 2 * int(round(VSHARE[h] * 2 * nb))] + [x * nb for x in CUTS]
+            cuts = [2 * int(round(VSHARE[h] * 2 * nb * x / VPARTS)) for x in range(VPARTS + 1)] + [x * nb for x in CUTS]
             ga = []
-            for a, b in zip(cuts, cuts[1:]):
+            for x, (a, b) in enumerate(zip(cuts, cuts[1:])):
                 need = [cv[0]] * (a < 2 * nb) + [cv[-1]] * (b > 2 * nb) + pyr
                 cells, out = win[:, 0:WIN].indirect(off[:, a:b]), gt[:, 16 * a:16 * b]
-                if a:
+                if x >= VPARTS:
                     ga.append(op("A", 65, need, lambda out=out, cells=cells: S.activation(out, cells, AF.Copy), ge=16 * (b - a)))
                 else:
                     ga.append(op("V", 50, need, lambda out=out, cells=cells: V.tensor_copy(out, cells), ge=16 * (b - a)))
-            cuts, ga = [0] + cuts[2:], [ga[0:2]] + [[x] for x in ga[2:]]
+            cuts, ga = [0] + cuts[VPARTS + 1:], [ga[0:VPARTS + 1]] + [[x] for x in ga[VPARTS + 1:]]
             pz = pa[0:24, 0:nb]
             z = mm(32, [cv[0], CZ], [(pz, T.cz[:, 0:24], src, True, False)])
             scs = []
@@ -496,14 +537,14 @@ def build(g, T, topo, core):
                     o, s = T.ft[:, n4:16:4, B0[i]:B0[i] + nb], sc[:, 4 * n4 + 3:64 * nb:16]
                     fo.append(act(4 * nb, scs, o, s) if n4 % 2 else v(2 * nb, scs, lambda o=o, s=s: V.tensor_copy(o, s)))
             n1 = ts(nb, [z, m1], sb[0:24, sa + 2:sa + 3 * nb:3], pz, 92160.0, 104448.0, A.max, A.min, late=-400)
-            mt, prev[i] = update(src, mb, 3 * h * nb, pa, pb, nb, [n1, cv[-1]], h == N - 1)
+            mt, prev[i] = update(src, mb, 3 * h * nb, pb, nb, [n1, cv[-1]])
             if h == N - 1:
                 hist = trail(i, range(N - 1), [n1], [mt])
                 to.append(act(nb, [trail(i, [h], [prev[i]], [hist])], T.tr[0:96, B0[i]:B0[i] + nb], pa[0:96, 0:nb]))
 
     op("Y", 3000, fo, lambda: Y.dma_start(T.feat[:], T.ft[:]), sem=("dft", 16))
     op("A", 2000, to, lambda: S.dma_start(T.trail[:], T.tr[0:96, :]), sem=("dtr", 16))
-    return ops, nsent[0]
+    return ops, nsent
 
 
 PLANS = []

import math
from concourse.bass import DstId, RemoteDMATransfer
from concourse.mybir import AluOpType as A, ActivationFunctionType as AF

N = 4
SIM = 112
BATCH = [22, 22, 20]
VSHARE = [0.24, 0.23, 0.24, 0.3]
VPARTS = 1
SPLIT = True
CUTS = [2, 3, 4]
SEG = 16 * max(BATCH) * max(b - a for a, b in zip([0] + CUTS, CUTS))
PLANFOR = [(1500, 1.2, 70., 130.), (0, 1.5, 100., 180.), (3000, 1.8, 70., 130.), (2500, 1.35, 130., 250.)]
STARTS, TRIES = 200, 130000
EARLY, LONG, HEAT = 4.5, 2.0, 40.0
AHEAD = 2
LOADED = [2700, 3600, 3100, 2700]
ARRIVE = [5000, 10000, 15000]
STEPS = ["win", "win1", "win2", "win3"]
COPIES = [(-h, STEPS[h]) for h in range(1, N)]
NBT = len(BATCH)
B0 = [sum(BATCH[:i]) for i in range(NBT)]
MV = [8256, 7168, 2080, 1984]
LV = [(0, 4096), (4096, 1024), (5120, 256), (5376, 64)]
WIN = MV[0] - MV[3] + 4096
SMALL = MV[2] - MV[3] + 256
PLAIN = [(far, False, i, i, False) for i in range(2) for far in (False, True)]
PORT = [(True, True, i, i, False) for i in range(2)]
LOW = (False, True, 0, 0, False)
OWN = (False, True, 0, 0, True)
CALLS = [(416, PLAIN), (352, PORT + [OWN]), (SMALL, [LOW] + PLAIN), (352, PORT + [OWN[:3] + (1, True)])]
PART = 420
PIECES = []
_a = MV[1] - MV[3]
for _j, (_w, _ps) in enumerate(CALLS):
    for _p in _ps:
        PIECES.append((_j, 0, _w) + _p if _p is LOW else (_j, _a, _a + _w) + _p)
        _a += 0 if _p is LOW else _w
HEADS = [LOW, PORT[0], PORT[1]]
THIN = [2, 2, 2]
UM = 160
NK = 14
KF, KF2, KU0, KU1, KV0, KV1, KCZ, KUP, KL1, KL2, KX, KY, KS, KC = range(NK)
KTAB = [(KF, 5, 1, 1, 0.5), (KF, 6, 1, 1, 0.25), (KF, 7, 2, 7 * NK, 0.125), (KF, 13, 1, 1, -38.0),
        (KF2, 5, 1, 1, 0.75), (KF2, 6, 1, 1, 0.1875), (KF2, 7, 1, 1, 3 / 64), (KF2, 13, 1, 1, -47.25), (KF2, 14, 1, 1, 1 / 64),
        (KU0, 8, 1, 1, 1.0), (KU0, 5, 1, 1, -160.0), (KU0, 6, 1, 1, -320.0), (KU0, 7, 1, 1, -640.0), (KU0, 2, 1, 1, 0.5),
        (KU0, 3, 1, 1, 1.0), (KU0, 4, 1, 1, 2.0), (KU0, 9, 1, 1, 32640.0), (KU0, 13, 1, 1, -102.0), (KU0, 14, 1, 1, 1 / 32),
        (KU1, 10, 1, 1, 1 / 16), (KV1, 10, 1, 1, 4.0),
        (KV0, 12, 1, 1, 64.0), (KV0, 5, 1, 1, -20352.0), (KV0, 6, 1, 1, -4544.0), (KV0, 7, 1, 1, -93696.0), (KV0, 2, 1, 1, -32.0),
        (KV0, 4, 1, 1, 128.0), (KV0, 9, 1, 1, 2867200.0), (KV0, 13, 1, 1, -1664.0), (KV0, 14, 1, 1, 2.0),
        (KCZ, 13, 1, 1, 12288.0), (KCZ, 14, 1, 1, -32.0), (KCZ, 15, 1, 1, 1 / 16),
        (KUP, 2, 2, 3 * NK, 53.0), (KUP, 3, 2, 3 * NK, 41.0), (KUP, 4, 2, 3 * NK, 17.0), (KUP, 8, 2, 4 * NK, 60.0), (KUP, 10, 1, 1, 56.0),
        (KL1, 5, 2, 1, 52.0), (KL1, 6, 2, 1, 40.0), (KL1, 7, 2, 1, 16.0), (KL1, 8, 2, 4 * NK, 8.0),
        (KL1, 2, 2, 1, 52.0), (KL1, 3, 2, 1, 40.0), (KL1, 4, 2, 1, 16.0), (KL1, 10, 2, 1, 4.0),
        (KUP, 9, 3, 1, 1.0), (KUP, 13, 3, 1, 1.0), (KUP, 14, 3, 1, 1.0), (KUP, 15, 3, 1, 1.0),
        (KX, 0, 3, NK + 1, 1 / 512), (KX, 14, 3, 1, -192.0), (KX, 8, 2, 2 * NK + 2, 1.0), (KY, 12, 1, 1, 1.0),
        (KC, 2, 1, 1, -1 / 512), (KC, 10, 1, 1, -1.0), (KC, 14, 1, 1, 256.0)]
NEWS = [[(0, 80, KC), (80, 96, KS), (96, 128, KC)], [(0, 64, KC), (64, 80, KX), (80, 96, KS), (96, 128, KY)]]

BF = "bfloat16"
SCRATCH = {"sxy": ("sbuf", [128, 16], "int32"), "bx": ("sbuf", [128, 64], "int32"), "pi": ("sbuf", [128, 4], "int32"),
           "kc": ("sbuf", [128, 16], "float32"), "pf": ("sbuf", [128, 4], "float32"), "mg": ("sbuf", [128, 8], "float32"),
           "tr": ("sbuf", [128, 64], "float32"), "ft": ("sbuf", [128, 16, 64], BF)}
for _k, _n in dict(krow=16 * NK, zrow=256, icol=128, jrow=128, grow=128, g8=80, mkl=128, tmpl=256, l1=256, fm=256, cz=32,
                   eg=256, pw=112, seg=SEG, i0=64, i1=192, lim=192).items():
    SCRATCH[_k] = ("sbuf", [128, _n], BF)
for _w in ["win"] + [_c[1] for _c in COPIES]:
    SCRATCH["wz" + _w] = ("sbuf", [128, 3, 128], BF)
    for _k, _n in (("", WIN), ("hd", 64), ("ot", 1024), ("oh", 1024)):
        SCRATCH[_k + _w] = ("sbuf", [128, _n], BF)
for _i, _nb in enumerate(BATCH):
    SCRATCH["pa%d" % _i] = ("psum", [128, 512], "float32")
    SCRATCH["pb%d" % _i] = ("psum", [128, 512], "float32")
    SCRATCH["mb%d" % _i] = ("sbuf", [128, N * 3 * _nb], BF)
    for _h in range(N):
        SCRATCH["off%d_%d" % (_h, _i)] = ("sbuf", [128, 4 * _nb], "uint16")
        for _k, _n in (("uv", 2), ("ff", 2), ("gt", 64), ("sc", 64)):
            SCRATCH["%s%d_%d" % (_k, _h, _i)] = ("sbuf", [128, _n * _nb], BF)
SEMAPHORES = (["cP", "cV", "cA", "cG", "dhd", "dsxy", "dbx", "dft", "dtr", "sent", "head"]
              + [x + c[1] for c in COPIES for x in ("small", "big")] + ["ch%d" % j for j in range(len(CALLS) + 1)]
              + ["dp%d" % (j + 1) for j in range(len(CALLS))] + ["dw" + w for w in STEPS[1:]]
              + ["rl%d_%d_%d" % (c, k, p) for c in range(N - 1) for k, x in enumerate(PIECES) for p in range(-(-(x[2] - x[1]) // PART))])
CY = 1.04


def plan(ops):
    n = len(ops)
    q = ["VAPGYX".index(o["q"]) for o in ops]
    pre = [set(o["deps"]) | set(o["after"]) for o in ops]
    cases = [([[(d, l1 if q[d] == q[k] else l2) for d in o["deps"]] + [(d, 0.) for d in o["after"]] for k, o in enumerate(ops)],
              [o["cost"] + o["ge"] * gc * CY + o["hp"] * hop for o in ops]) for hop, gc, l1, l2 in PLANFOR]
    tail = [o["tail"] for o in ops]
    urge = [k for k, o in enumerate(ops) if o["sem"] == ()][:len(CALLS) + 1]

    def replay(order, case):
        dep, cost = case
        end, why, res, free, last = [0.] * n, [-1] * n, [False] * n, [0.] * 6, [-1] * 6
        for k in order:
            e = q[k]
            t, w, r = free[e], last[e], True
            for d, l in dep[k]:
                if end[d] + l > t:
                    t, w, r = end[d] + l, d, False
            end[k], why[k], res[k] = t + cost[k], w, r
            if e != 5:
                free[e], last[e] = end[k] - tail[k], k
        return end, why, res

    seed = [12345]

    def rnd():
        seed[0] = (seed[0] * 1103515245 + 12345) % 2147483648
        return (seed[0] >> 8) / 8388608.0

    def value(o):
        r = [replay(o, c) for c in cases]
        return sum(max(x[0]) + sum(0.2 * x[0][k] for k in urge) for x in r) / len(r), r

    suc = [[] for _ in ops]
    for k in range(n):
        for d in pre[k]:
            suc[d].append(k)
    first = []
    for it in range(STARTS):
        dep, cost = cases[it % len(cases)]
        rest = [0.] * n
        for k in reversed(range(n)):
            rest[k] += cost[k]
            for d, l in dep[k]:
                rest[d] = max(rest[d], rest[k] + l)
        win, noise, step = 300 * rnd(), 300 * rnd(), (1e5, 1e3, 500.)[int(rnd() * 3)]
        pri = [1e9 - k if tail[k] or k in urge else 0.2 * rest[k] + noise * rnd() - step * ops[k]["turn"] - LONG * cost[k] for k in range(n)]
        left = [len(p) for p in pre]
        ready = {k: 0. for k in range(n) if not left[k]}
        end, free, o = [0.] * n, [0.] * 6, []
        while ready:
            st = {k: max(t, free[q[k]]) for k, t in ready.items()}
            k0 = min(st, key=st.get)
            k = max((x for x in st if q[x] == q[k0] and st[x] <= st[k0] + win), key=lambda x: pri[x])
            end[k] = st[k] + cost[k]
            if q[k] != 5:
                free[q[k]] = end[k] - tail[k]
            o.append(k)
            del ready[k]
            for s in suc[k]:
                left[s] -= 1
                if not left[s]:
                    ready[s] = max(end[d] + l for d, l in dep[s])
        first.append((value(o)[0], o))
    first.sort()
    low, kept = first[0]

    def critical(runs):
        out = []
        for end, why, res in runs:
            k = end.index(max(end))
            while k >= 0:
                if res[k] and why[k] >= 0 and why[k] not in pre[k]:
                    out.append(k)
                k = why[k]
        return out

    def again(o, pa, bound):
        seen, tot, new, rest = {q[k]: k for k in o[:pa]}, 0., [], o[pa:]
        for i, (dep, cost) in enumerate(cases):
            end, free = ends[i][:], [0.] * 6
            for e, k in seen.items():
                free[e] = (end[k] - tail[k]) * (e != 5)
            new.append(end)
            for k in rest:
                e = q[k]
                t = free[e]
                for d, l in dep[k]:
                    if end[d] + l > t:
                        t = end[d] + l
                end[k] = t = t + cost[k]
                if e != 5:
                    free[e] = t - tail[k]
            tot += max(end) + sum(0.2 * end[k] for k in urge) - olds[i]
            if tot > bound + 150. * (len(cases) - 1 - i):
                return None
        return new

    def each(ends):
        return [max(x) + sum(0.2 * x[k] for k in urge) for x in ends]

    order = kept
    ends = [x[0] for x in value(order)[1]]
    olds = each(ends)
    for it in range(TRIES):
        heat = HEAT * (1 - it / TRIES)
        if it % 16 == 0:
            crit = critical([replay(order, cases[it // 16 % len(cases)])])
        b = crit[int(rnd() * len(crit))] if crit and rnd() > 0.25 else order[int(rnd() * n)]
        pb = order.index(b)
        same = [x for x in order[max(0, pb - 40):pb] if q[x] == q[b]]
        if q[b] >= 4 or not same:
            continue
        a = same[-min(len(same), (1, 1, 1, 2, 3, 5)[int(rnd() * 6)])]
        if ops[a]["tail"] > 1000:
            continue
        pa = order.index(a)
        seg = order[pa:pb + 1]
        if rnd() < 0.5:
            grp = {b}
            for x in reversed(seg[:-1]):
                if any(x in pre[y] for y in grp):
                    grp.add(x)
            new = [x for x in seg if x in grp] + [x for x in seg if x not in grp]
        else:
            grp = {a}
            for x in seg[1:]:
                if pre[x] & grp:
                    grp.add(x)
            new = [x for x in seg if x not in grp] + [x for x in seg if x in grp]
        if a in grp and b in grp:
            continue
        o2 = order[:pa] + new + order[pb + 1:]
        got = again(o2, pa, -len(cases) * (heat + 3) * math.log(rnd() + 1e-9))
        if got:
            order, ends, olds = o2, got, each(got)
            cur = sum(olds) / len(olds)
            if cur < low:
                low, kept = cur, order
    return kept, [max(replay(kept, c)[0]) for c in cases], replay(kept, cases[1])[0]


def holder(src, k, c, T, topo):
    return src if PIECES[k][7] and not c else held_by(src, PIECES[k][3:], T, topo)


def held_by(src, entry, T, topo):
    far, port, idx = entry[:3]
    other = T.cores[(T.rank_of(src) + 1) % N]
    return [x for x in topo.cores_of(src) if x != src and (topo.die(x) != topo.die(src)) == far and topo.may_write(x, other) == port][idx]


def relay(src, dst, k, T, topo):
    j, a, b, far, port, idx, hand, spare = PIECES[k]
    if port != topo.same_plane(topo.chip(src), topo.chip(dst)):
        return None
    return [y for y in range(SIM) if topo.mates(topo.chip(y), topo.chip(dst)) and (topo.die(y) != topo.die(src)) == far
            and topo.may_write(y, dst)][hand]


def call_engines(src, j, T, topo):
    ks = [k for k, p in enumerate(PIECES) if (p[0] == j if j < len(CALLS) else p[7])]
    every, off = topo.engines(src, holder(src, 0, 0, T, topo)), topo.engines(src, T.cores[(T.rank_of(src) + 1) % N])
    own = [k for k in ks if PIECES[k][7] and j < len(CALLS)]
    near, far = ([k for k in ks if k not in own and PIECES[k][3] == x] for x in (False, True))
    rest = [e for e in every if e not in off or not own]
    sets = [(own, off)] * bool(own) + ([(near, rest[1::2]), (far, rest[0::2])] if near and far else [(near + far, rest)])
    out = {}
    for x, eng in sets:
        share = 1 << (len(x) - 1).bit_length()
        for i, k in enumerate(x):
            out[k] = eng[i * len(eng) // share:(i + 1) * len(eng) // share if i + 1 < len(x) else None]
    return out


def thin(c, k):
    return 1 if c == 0 and PIECES[k][4] else 2


def parts(k, via):
    return 1 if via is None else -(-(PIECES[k][2] - PIECES[k][1]) // PART)


def helper(g, core, T, topo):
    n = 0
    for c, (d, wn) in enumerate(COPIES):
        for r in range(N):
            src, dst = T.cores[r], T.cores[(r + d) % N]
            if core == held_by(src, HEADS[c], T, topo):
                g.wait_ge(T.sem.head, len(topo.engines(src, core)[c::4]))
                g.remote_dma(T["hd" + wn][:], T.hdwin[:], T.sem["small" + wn], T.sem.sent, topo.addr(dst)[1], topo.addr(dst)[0], topo.mask(core, dst))
                n += len(topo.engines(core, dst))
    for c, (d, wn) in enumerate(COPIES):
        for r in range(N):
            src, dst = T.cores[r], T.cores[(r + d) % N]
            for k in range(len(PIECES)):
                j, a, b, far = PIECES[k][:4]
                via = relay(src, dst, k, T, topo)
                held = core == holder(src, k, c, T, topo)
                if not held and core != via:
                    continue
                to = via if held and via is not None else dst
                eng = topo.engines(core, to)[::thin(c, k)]
                if held and c == 0:
                    g.wait_ge(T.sem["ch%d" % j], sum(len(e) for x, e in call_engines(src, j, T, topo).items() if holder(src, x, 0, T, topo) == core))
                if held and c == 1 and PIECES[k][7]:
                    g.wait_ge(T.sem["ch%d" % len(CALLS)], sum(len(e) for e in call_engines(src, len(CALLS), T, topo).values()))
                m = parts(k, via)
                for p in range(m):
                    lo, hi, stop = a + (b - a) * p // m, a + (b - a) * (p + 1) // m, "rl%d_%d_%d" % (c, k, p)
                    if not held:
                        g.wait_ge(T.sem[stop], len(eng))
                    g.remote_dma(T[wn][:, lo:hi], T["win" if held else wn][:, lo:hi], T.sem[stop if to != dst else "big" + wn],
                                 T.sem.sent, topo.addr(to)[1], topo.addr(to)[0], sum(1 << e for e in eng))
                    n += len(eng)
    if n:
        g.wait_ge(T.sem.sent, n)


def build(g, T, topo, core):
    V, S, P, Y = g.vector, g.scalar, g.tensor, g.sync
    ops = []
    turn = [-NBT - 1]
    rank = T.rank_of(core)

    def peer(d):
        return T.cores[(rank + d) % N]

    def op(q, cost, deps, fn, late=0.0, sem=None, after=(), tail=0.0, ge=0, hp=0, drain=False):
        ops.append(dict(q=q, cost=float(cost), deps=list(deps), fn=fn, late=late, sem=sem, after=list(after), tail=tail,
                        ge=ge, hp=hp, drain=drain, turn=turn[0]))
        return len(ops) - 1

    def v(n, deps, fn, late=0.0):
        return op("V", max(64, n) * CY, deps, fn, late)

    def act(n, deps, out, in_, scale=1.0, late=0.0):
        return op("A", max(64, n) * CY, deps, lambda: S.activation(out, in_, AF.Copy, scale=scale), late)

    def ts(n, deps, *a, late=0.0):
        return v(n, deps, lambda: V.tensor_scalar(*a), late)

    def fill(n, ap, val, deps=(), late=0.0):
        return v(n, deps, lambda: V.memset(ap, val), late)

    def mm(n, deps, calls, after=()):
        def fn():
            r = None
            for c in calls:
                r = P.matmul(*c)
            return r
        return op("P", n * CY, deps, fn, after=after)

    def load(q, out, in_, sem, cost, deps=()):
        return op(q, cost, deps, lambda: (S if q == "A" else Y).dma_start(out, in_), -1e4, sem=sem, tail=cost - 100)

    kc = T.kc

    def col(k):
        return kc[:, k:k + 1]

    load("A", T.sxy[:, 0:4], T.sx[:], ("dsxy", 16), 2000)
    dsy = load("A", T.sxy[:, 4:8], T.sy[:], ("dsxy", 32), 2000)
    dhd = load("A", T.hdwin[:, 0:48], T.head[:], ("dhd", 16), 2000)
    for e in range(3):
        dbx = load("A", T.bx[8 * e:8 * e + 8, :], T.box[:, 64 * e:64 * e + 64], ("dbx", 16 * (e + 1)), 2000)
    dps = []
    for j in range(len(CALLS)):
        mine, n = [p for p in PIECES if p[0] == j], 0
        lo, hi = min(p[1] for p in mine if p[1]), max(p[2] for p in mine)
        for l in range(4):
            a, b = MV[l] - MV[3], MV[l] - MV[3] + LV[l][1]
            a, b = (max(lo, a), min(hi, b)) if l < 2 else (a, b * (LOW in CALLS[j][1]))
            if a < b:
                n += 1
                o = LV[l][0] - MV[l] + MV[3]
                dp = load("Y", T.win[:, a:b], T.pyr[:, a + o:b + o], ("dp%d" % (j + 1), 16 * n), LOADED[j], dps[-AHEAD:1 - AHEAD])
        dps.append(dp)

    zk = fill(8 * NK, T.krow[0:1, :], 0.0, late=-600)
    zo = fill(64, T.zrow[0:1, 120:128], 1.0, late=-600)
    ks = [zo, fill(64, T.zrow[0:1, 0:120], 0.0), fill(64, T.zrow[0:1, 128:256], 0.0)]
    for j, (k, a, n, st, val) in enumerate(KTAB):
        ap = T.krow[0:1, a * NK + k:a * NK + k + (n - 1) * st + 1:st]
        if j % 2:
            ks.append(act(1, [zk, zo], ap, T.zrow[0:1, 120:120 + n], val))
        else:
            ks.append(fill(1, ap, val, [zk], -200))
    mk = mm(1024, ks, [(T.pa0[:, 0:NK], T.zrow[0:1, 120 - 8 * t:248 - 8 * t], T.krow[0:1, t * NK:(t + 1) * NK], t == 0, t == 15)
                       for t in range(16)])

    lastg = []

    def gi(ap, pat, base, cm, val=None, deps=(), after=()):
        n = math.prod(c for _, c in pat)
        if val is None:
            def fn():
                return g.iota(ap, pat, base, cm, allow_small_or_imprecise_dtypes=True)
        else:
            def fn():
                return g.affine_select(ap, ap, pat, A.not_equal, val, base, cm)
        lastg[:] = [op("G", 150 + 2 * n * CY, list(deps) + lastg, fn, after=after)]
        return lastg[0]

    eg = T.eg
    ipi = gi(T.pi[:, 0:1], [[0, 1]], 0, 1)
    iic = gi(T.icol[:], [[1, 128]], 0, 0)
    ig8 = gi(T.g8[:], [[0, 10], [1, 8]], 0, 0)
    ijr = gi(T.jrow[:], [[0, 8], [1, 16]], 0, 0)
    igr = gi(T.grow[:], [[1, 8], [0, 16]], 0, 0)
    iseg = fill(SEG / 8, T.seg[:, 0:SEG:4], 0.0, [fill(SEG / 2, T.seg[:], 256.0, late=1000)], 1000)

    p1 = ts(1, [ipi], T.pi[:, 1:2], T.pi[:, 0:1], 7, None, A.bitwise_and)
    p2 = ts(1, [ipi], T.pi[:, 2:3], T.pi[:, 0:1], 112, None, A.bitwise_and)
    p3 = v(1, [p1, p2], lambda: V.tensor_copy(T.pf[:, 1:3], T.pi[:, 1:3]))
    pm8, p16 = T.pf[:, 1:2], T.pf[:, 2:3]
    oi = fill(64, T.i0[:], 1.0)
    kcp = v(64, [mk], lambda: V.tensor_copy(kc[:, 0:NK], T.pa0[:, 0:NK]), -500)
    LIM = [ts(1, [kcp, iic], T.lim[:, t:192:3], T.icol[:, 0:64], 0.0, col(KUP + t), A.mult, A.add) for t in range(3)]
    ZB = [fill(64, T["pb%d" % i][:, 256:448:3], 0.0) for i in range(NBT)]
    d0 = ts(64, [dbx, oi], T.i0[0:24, :], T.bx[0:24, :], 191.0, 512.0, A.add, A.mult, late=-500)
    FM = [ts(64, [kcp, p3, igr], T.fm[:, 128 * j:128 * j + 128], T.grow[:], pm8, col(k), A.is_equal, A.mult) for j, k in enumerate((KF, KF2))]
    EG = [ts(1, [kcp, p3, ig8], eg[:, 128 * t + a:128 * t + b], T.g8[:, 0:b - a], pm8, col(k), A.is_equal, A.mult, late=-500)
          for t in range(2) for a, b, k in NEWS[t]]
    ml = ts(64, [p3, igr], T.mkl[:], T.grow[:], pm8, None, A.is_equal)
    L1 = []
    for j, (k0, k1) in enumerate(((KU0, KU1), (KV0, KV1))):
        tm = T.tmpl[:, 128 * j:128 * j + 128]
        t1 = ts(64, [kcp, ijr], tm, T.jrow[:], col(k1), col(k0), A.mult, A.add)
        L1.append(v(256, [t1, ml], lambda j=j, tm=tm: V.tensor_tensor(T.l1[:, 128 * j:128 * j + 128], tm, T.mkl[:], A.mult)))
    sco = ts(8, [dsy, p3], T.hdwin[:, 48:56], T.sxy[:, 0:8], p16, None, A.add)
    CZ = ts(24, [kcp, iic], T.cz[:, 0:24], T.icol[:, 0:24], 0.0, col(KCZ), A.mult, A.add)
    mgk = ts(8, [p3, iic], T.mg[:], T.icol[:, 0:128:16], p16, None, A.is_equal)

    def frame(wn, d1, d2, pyr, late):
        win, hd, ot, oh, wz = T[wn], T["hd" + wn], T["ot" + wn], T["oh" + wn], T["wz" + wn]
        ots = [ts(64, [d1, iic], ot[:, 128 * j:128 * j + 128], T.icol[:], hd[:, 48 + j:49 + j], None, A.is_equal, late=late)
               for j in range(8)]
        o = [v(128, ots[2 * j:2 * j + 2], lambda j=j: V.transpose(oh[:, 256 * j:256 * j + 256], ot[:, 256 * j:256 * j + 256]), late)
             for j in range(4)]
        if wn == STEPS[0]:
            return win, oh, wz, o, [act(48, [mgk, d2], wz[:, :, 16 * j:16 * j + 16], hd[:, 0:48], T.mg[:, j:j + 1]) for j in range(8)], pyr
        zero = act(384, [iseg], wz[:], T.seg[:, 0:384], 0.0)
        ops[zero]["turn"] = -NBT - 0.5
        for j in range(8):
            w = op("Y", 2000, [zero, d2], lambda j=j: Y.dma_start(wz[16 * j:16 * j + 16, :, 16 * j:16 * j + 16], hd[16 * j:16 * j + 16, 0:48]),
                   sem=("dw" + wn, 16 * (j + 1)), tail=1900)
        return win, oh, wz, o, [w], pyr

    gaps = [fill((b - a) / 2, T.win[:, a:b], 0.0, late=-300)
            for a, b in ((LV[3][1], MV[2] - MV[3]), (MV[1] - MV[3] + LV[1][1], MV[0] - MV[3]))]
    zh = fill(1, T.hdwin[:, 56:64], 0.0)
    frames = {"win": frame("win", sco, dhd, gaps + dps, 0.0)}

    def send(j):
        trs = []
        for k, eng in call_engines(core, j, T, topo).items():
            to, wn, sem = holder(core, k, j == len(CALLS), T, topo), "win", "ch%d" % j
            if to == core:
                to, wn, sem = peer(COPIES[0][0]), COPIES[0][1], "big" + COPIES[0][1]
            rid, pid, _ = topo.addr(to)
            a, b = PIECES[k][1:3]
            trs.append(RemoteDMATransfer(dst_ids=[DstId(rid=rid, pnc=pid)], dma_engine_mask=sum(1 << e for e in eng),
                                         remote_sem=T.sem[sem], src=T.win[:, a:b], dst=T[wn][:, a:b]))
        return g.remote_dma_fused(trs, local_sem=T.sem.sent)

    def heads():
        to = [held_by(core, x, T, topo) for x in HEADS]
        return g.remote_dma_fused([RemoteDMATransfer(dst_ids=[DstId(rid=topo.addr(x)[0], pnc=topo.addr(x)[1])], remote_sem=T.sem.head,
                                                     dma_engine_mask=sum(1 << e for e in topo.engines(core, x)[c::4]), src=T.hdwin[:], dst=T.hdwin[:])
                                   for c, x in enumerate(to)], local_sem=T.sem.sent)

    last = [op("G", 700, [dhd, sco, zh], heads, sem=(), after=[igr])]
    nsent = sum(len(topo.engines(core, held_by(core, x, T, topo))[c::4]) for c, x in enumerate(HEADS))
    for j in range(len(CALLS) + 1):
        last.append(op("G", 700, dps[j:j + 1] + gaps, lambda j=j: send(j), sem=(), after=last[-1:]))
        nsent += sum(len(e) for e in call_engines(core, j, T, topo).values())
    later = last[-1]
    for c, (d, wn) in enumerate(COPIES):
        ne = len(topo.engines(peer(-d), core))
        small, place = (op("X", t, [], None, sem=("small" + wn, ne), after=last[:1]) for t in (6500, 7500 + 4000 * c))
        big = op("X", ARRIVE[c], [], None, sem=("big" + wn, sum(len(call_engines(core, p[0], T, topo)[k]) if p[7] and not c else
                                                                 ne // thin(c, k) * parts(k, relay(peer(-d), core, k, T, topo))
                                                                 for k, p in enumerate(PIECES))), after=[last[len(CALLS)]], hp=1)
        turn[0] = (c + 1) * NBT - EARLY
        frames[wn] = frame(wn, small, place, [big], 400.0)
        turn[0] = -NBT - 1
    zp = fill(64, T.pw[:], 0.0, late=4000)
    for e, o in ((0, 0), (1, 32), (2, 16)):
        PW = gi(T.pw[64:128, 9 + e:105:12], [[-1, 8]], -o, 1, 1.0, [zp], [later])

    def update(src, dst, a, pb, nb, deps):
        mt = mm(128, deps + EG + ZB, [(pb[:, 257 + t:256 + 3 * nb:3], eg[:, 128 * t:128 * t + 128], src, True, True) for t in range(2)])
        new = v(3 * nb, [mt] + LIM, lambda: V.tensor_tensor_scan(dst[:, a:a + 3 * nb], pb[:, 256:256 + 3 * nb], T.lim[:, 0:3 * nb],
                                                                 0.0, A.min, A.max))
        return mt, new

    init = update(T.i0[:], T.i1, 0, T.pb0, 64, [d0])[1]

    prev = [init] * NBT
    mbs = [T["mb%d" % i] for i in range(NBT)]
    fo, to = [], []

    def trail(i, hs, deps, after):
        nb = BATCH[i]
        return mm(64 * len(hs), deps + [PW], [(T["pa%d" % i][0:96, 0:nb], T.pw[:, 9 - 3 * h:105 - 3 * h],
                                               mbs[i][:, 3 * h * nb + 2:3 * (h + 1) * nb:3], h == 0, h == N - 1) for h in hs], after)

    for h in range(N):
        win, oh, wz, OH, WZ, pyr = frames[STEPS[h]]
        for i, nb in enumerate(BATCH):
            pa, pb, mb = T["pa%d" % i], T["pb%d" % i], mbs[i]
            uv, off, gt, sc = (T["%s%d_%d" % (x, h, i)] for x in ("uv", "off", "gt", "sc"))
            sb, sa = (T.i1, 3 * B0[i]) if h == 0 else (mb, 3 * (h - 1) * nb)
            src = sb[:, sa + 2:sa + 3 * nb:3]
            turn[0] = (h - 1) * NBT + i
            ff = T["ff%d_%d" % (h, i)]
            mf, m1 = (mm(128, [prev[i]] + w, [(ps[:, c * nb:(c + 1) * nb], t[:, 128 * c:128 * c + 128], src, True, True) for c in range(2)])
                      for ps, t, w in ((pa, T.fm, FM), (pb, T.l1, L1)))
            fs = v(2 * nb, [mf], lambda ff=ff, pa=pa, nb=nb: V.tensor_copy(ff[:], pa[:, 0:2 * nb]))
            rd = v(2 * nb, [m1, fs], lambda uv=uv, pb=pb, ff=ff, nb=nb: V.tensor_tensor(uv[:], pb[:, 0:2 * nb], ff[:], A.mult))
            cv = []
            for ps, qs in ((pa, (0, 1)), (pb, (2, 3))) if SPLIT else ((pa, (0, 1, 2, 3)),):
                m2 = []
                for k, x in enumerate(qs):
                    m2 = [mm(128, [rd, OH[x // 2], OH[2 + x // 2]],
                             [(ps[:, k * nb:(k + 1) * nb], oh[:, 512 * c + 128 * x:512 * c + 128 * x + 128], uv[:, c * nb:(c + 1) * nb], c == 0, c == 1)
                              for c in range(2)], m2)]
                cv.append(ts(len(qs) * nb, m2, off[:, qs[0] * nb:(qs[-1] + 1) * nb], ps[:, 0:len(qs) * nb], -float(UM + MV[3]), None, A.add))
            turn[0] = h * NBT + i
            cuts = [2 * int(round(VSHARE[h] * 2 * nb * x / VPARTS)) for x in range(VPARTS + 1)] + [x * nb for x in CUTS]
            ga = []
            for x, (a, b) in enumerate(zip(cuts, cuts[1:])):
                need = [cv[0]] * (a < 2 * nb) + [cv[-1]] * (b > 2 * nb) + pyr
                cells, out = win[:, 0:WIN].indirect(off[:, a:b]), gt[:, 16 * a:16 * b]
                if x >= VPARTS:
                    ga.append(op("A", 65, need, lambda out=out, cells=cells: S.activation(out, cells, AF.Copy), ge=16 * (b - a)))
                else:
                    ga.append(op("V", 50, need, lambda out=out, cells=cells: V.tensor_copy(out, cells), ge=16 * (b - a)))
            cuts, ga = [0] + cuts[VPARTS + 1:], [ga[0:VPARTS + 1]] + [[x] for x in ga[VPARTS + 1:]]
            pz = pa[0:24, 0:nb]
            z = mm(32, [cv[0], CZ], [(pz, T.cz[:, 0:24], src, True, False)])
            scs = []
            for a, b, ks in zip(cuts, cuts[1:], ga):
                scs.append(v(8 * (b - a), ks + [iseg], lambda a=16 * a, b=16 * b, gt=gt, sc=sc:
                             V.tensor_tensor_scan(sc[:, a:b], T.seg[:, 0:b - a], gt[:, a:b], 0.0, A.min, A.max)))
                z = mm(4 * (b - a) // nb * max(24, nb), scs[-1:] + WZ,
                       [(pz, wz[:, :, n:128:16], sc[:, 16 * nb * (n // 4) + 4 * (n % 4) + 3:16 * nb * (n // 4 + 1):16], False, n == 15)
                        for n in range(4 * a // nb, 4 * b // nb)], after=[z])
            if h == N - 1:
                for n4 in range(4):
                    o, s = T.ft[:, n4:16:4, B0[i]:B0[i] + nb], sc[:, 4 * n4 + 3:64 * nb:16]
                    fo.append(act(4 * nb, scs, o, s) if n4 % 2 else v(2 * nb, scs, lambda o=o, s=s: V.tensor_copy(o, s)))
            n1 = ts(nb, [z, m1], sb[0:24, sa + 2:sa + 3 * nb:3], pz, 92160.0, 104448.0, A.max, A.min, late=-400)
            mt, prev[i] = update(src, mb, 3 * h * nb, pb, nb, [n1, cv[-1]])
            if h == N - 1:
                hist = trail(i, range(N - 1), [n1], [mt])
                to.append(act(nb, [trail(i, [h], [prev[i]], [hist])], T.tr[0:96, B0[i]:B0[i] + nb], pa[0:96, 0:nb]))

    op("Y", 3000, fo, lambda: Y.dma_start(T.feat[:], T.ft[:]), sem=("dft", 16))
    op("A", 2000, to, lambda: S.dma_start(T.trail[:], T.tr[0:96, :]), sem=("dtr", 16))
    return ops, nsent


PLANS = []


def rank_program(g, core, T, topo):
    if T.rank_of(core) is None:
        helper(g, core, T, topo)
        return
    ops, nsent = build(g, T, topo, core)
    if not PLANS:
        PLANS.append(plan(ops)[0])
    order = PLANS[0]
    Q = {"V": g.vector, "A": g.scalar, "P": g.tensor, "G": g, "Y": g.sync}
    needed = set(d for o in ops for d in o["deps"])
    sig = {}
    count = {}
    for k in order:
        o = ops[k]
        if o["sem"] is None:
            if k in needed:
                s = "c" + o["q"]
                count[s] = count.get(s, 0) + 1
                sig[k] = (s, count[s])
        elif o["sem"]:
            sig[k] = o["sem"]
            count[o["sem"][0]] = max(count.get(o["sem"][0], 0), o["sem"][1])
    seen = {}
    drain = []
    for k in order:
        o = ops[k]
        if o["q"] == "X":
            continue
        want = {}
        for d in o["deps"] + (drain if o["q"] == "V" else []):
            s, n = sig[d]
            want[s] = max(want.get(s, 0), n)
        for s in sorted(want):
            if seen.get((o["q"], s), 0) < want[s]:
                Q[o["q"]].wait_ge(T.sem[s], want[s])
                seen[(o["q"], s)] = want[s]
        r = o["fn"]()
        if o["q"] == "V":
            drain = [k] if o["drain"] else []
        if k in sig:
            r.then_inc(T.sem[sig[k][0]], 1 if o["sem"] is None else 16)
    count["sent"] = nsent
    for s in sorted(count):
        if not any(seen.get((q, s), 0) >= count[s] for q in Q):
            g.sync.wait_ge(T.sem[s], count[s])
